import numpy as np, ml_dtypes
CORES = [66,74,82,90,194,202,210,218]
N = 8
import mx_ref
BF = ml_dtypes.bfloat16
def gentries(a):
    return np.ascontiguousarray(a.reshape(8, 16, -1).transpose(0, 2, 1)).reshape(8, -1)
def gtable(e):
    e = np.asarray(e); return np.ascontiguousarray(e.reshape(8, -1, 16).transpose(0, 2, 1)).reshape(128, -1).astype(np.int32)
def tile(rs):
    return np.stack(rs, axis=2).reshape(128, -1).astype(BF)
def pick(q, e):
    c = np.concatenate([q[0].reshape(128, -1, 4), np.zeros((128, 1, 4), np.uint8)], axis=1); s = np.concatenate([q[1], np.ones((16, 1), np.uint8)], axis=1)
    return (np.ascontiguousarray(c[:, e].reshape(128, -1)), np.ascontiguousarray(s[:, e]))
def join(*qs):
    return (np.concatenate([q[0] for q in qs], axis=1), np.concatenate([q[1] for q in qs], axis=1))
def put(q, e, v):
    c, s = q[0].reshape(128, -1, 4).copy(), q[1].copy(); c[:, e] = v[0].reshape(128, -1, 4); s[:, e] = v[1]
    return (c.reshape(128, -1), s)
def pk(c, s):
    return (np.ascontiguousarray(c), mx_ref.live(s))
def emit(q):
    return q[0], q[1]
def packed(v, rng):
    q = [mx_ref.quantize(np.ascontiguousarray(v[r])) for r in range(N)]
    return np.stack([a for a, b in q]), np.stack([mx_ref.plane(b, rng) for a, b in q])
def values_of_codes():
    e, c = np.zeros((128, 128, 4), np.float32), np.zeros((128, 2, 4), np.uint8)
    e[np.arange(128), np.arange(128), 0] = 1
    c[:127, :, 0] = np.arange(256).reshape(2, 128).T[:127]
    return mx_ref.matmul(mx_ref.quantize(e.reshape(128, 512).astype(BF)), (c.reshape(128, 8), np.full((16, 2), 127, np.uint8))).T.reshape(-1).astype(np.float64)
CODE_VALUE, SCALE_VALUE = values_of_codes(), 2.0 ** (np.arange(256) - 127.0)
def decode(q):
    return (CODE_VALUE[q[0]].reshape(16, 8, -1, 4) * SCALE_VALUE[q[1]][:, None, :, None] + 0.0).reshape(128, -1).astype(np.float32)
def f(rng, *shape):
    return mx_ref.flush((rng.standard_normal(shape, dtype=np.float32) * np.exp2(rng.integers(-2, 3, shape[:-1] + (1,)))).astype(BF))
def wide(rng, *shape, cols=0):
    v = rng.standard_normal(shape, dtype=np.float32) * np.exp2(rng.integers(-12, 13, shape)).astype(np.float32)
    if cols: v *= np.repeat(np.exp2(rng.integers(-cols, cols + 1, shape[:-2] + (1, shape[-1] // 4))) * (rng.random(shape[:-2] + (1, shape[-1] // 4)) > 0.0625), 4, axis=-1).astype(np.float32)
    return mx_ref.flush(v.astype(BF))
C, B, L, M, R = 288, 48, 384, 128, 3
MASK = [1, 2, 4]
def big(v):
    v = v.astype(np.float32)
    v[np.abs(v) < np.float32(2.0 ** -16)] = 0
    return v.astype(BF)
def numbers_of(rng):
    return {"x": big(f(rng, N, 128, 4 * C)), "u": np.array(f(rng, N, 128, 512)), "v": np.array(f(rng, N, 128, 512))}
def rings(rng, ends=False):
    p = [np.arange(C)[::1 - 2 * (h % 2)] if ends else rng.permutation(C) for h in range(8)]
    e = np.zeros((8, L), np.int64)
    for g in range(8):
        a, b = (g - 1) % 8, (g + 1) % 8
        e[g] = rng.permutation(np.concatenate([C * g + np.arange(C), C * a + p[a][:B], C * b + p[b][B:2 * B]]))
        if ends: e[g] = np.sort(e[g])[::1 - 2 * (g // 2 % 2)]
    return np.stack([gtable(e)] * N)
def layers(rng):
    return big(np.clip(f(rng, N, 128, 2048).astype(np.float32) * np.float32(0.25), -1.75, 1.75)).reshape(N, 8, 16, 4, 8, 16, 4)
def weights(rng, w):
    c, s = packed(np.ascontiguousarray(w).reshape(N, 128, 2048), rng)
    return {"wc": c, "ws": s}
def setup_inputs(rng):
    return {**numbers_of(rng), "ring": rings(rng), **weights(rng, layers(rng))}
def setup_inputs_ties(rng):
    d = numbers_of(rng)
    o = rng.permutation(N)
    same = rng.random((N, 8, C)) < rng.random((N, 8, 1))
    same[o[0]] = True
    same[o[0], rng.integers(8)] = False
    a = rng.integers(0, 3, (N, 8, C))
    b = np.where(same, a, rng.integers(0, 3, (N, 8, C)))
    least = max(257 if C > 256 else 0, 17 * C // 20) | 1
    for r in o[1:]:
        n = rng.permutation(np.arange(least, 19 * C // 20 + 1, 2))[:3]
        for i, g in enumerate(rng.permutation(8)[:3]):
            b[r, g] = a[r, g]
            j = rng.permutation(C)[:n[i]]
            more = rng.integers(1, 3, n[i])
            less = rng.integers(0, more)
            a[r, g, j] = more if o[r] % 2 else less
            b[r, g, j] = less if o[r] % 2 else more
    x = d["x"].reshape(N, 8, 16, C, 4)
    x[:, :, 0] = 0
    x[:, :, 0, :, 0] = a.astype(np.float32).astype(BF)
    x[:, :, 0, :, 1] = b.astype(np.float32).astype(BF)
    u = d["u"].reshape(N, 128, 128, 4)
    u[:, :, ::16] = 0
    for r in range(N):
        for h in range(0, 128, 16):
            u[r, h, h, 0] = 1.0 if o[r] % 2 else -1.0
            u[r, h, h, 1] = -1.0 if o[r] % 2 else 1.0
    w = layers(rng)
    w[:, :, :, :, :, 0] = 0
    return {"x": x.reshape(N, 128, 4 * C), "u": u.reshape(N, 128, 512), "v": d["v"], "ring": rings(rng), **weights(rng, w)}
def setup_inputs_near(rng):
    d = numbers_of(rng)
    o = rng.permutation(N) % 4
    k = rng.integers(0, 4, (N, 8, C))
    a = np.array([1.125, -1.125, 1.0, -1.0])[k]
    b = np.array([-1.25, 1.25, -1.125, 1.125])[k]
    x = d["x"].astype(np.float32).reshape(N, 8, 16, C, 4)
    x[:, :, :8] = 0
    u = d["u"].reshape(N, 128, 128, 4)
    u[:, :, ::16] = 0
    i = np.arange(32)
    s = np.exp2(-12.0 - i // 2 % 4)
    for r in range(N):
        z = 2.0 ** -30 if o[r] < 2 else 1.0
        x[r, :, 0, :, 0] = a[r] * z
        x[r, :, 1, :, 0] = b[r] * z
        for g in range(8):
            j = rng.permutation(C)[:32]
            x[r, g, 0, j, 0] = 0
            x[r, g, 1, j, 0] = 0
            x[r, g, 2, j, 0] = 1.96875
            x[r, g, 3, j, 0] = np.where(i % 2 == 0, 1.5, 1.125) * s
            x[r, g, 4, j, 0] = np.where(i % 2 == 0, -1.375, -1.0) * s
        for g in rng.permutation(8)[:4]:
            j = rng.integers(C)
            x[r, g, :8, j] = 0
            x[r, g, 0, j, 0] = 2.0 ** 14 * rng.choice([-1.0, 1.0])
        for h in range(0, 128, 16):
            z = 2.0 ** -30 if o[r] % 2 == 0 else 1.0
            u[r, h, h, 0] = 1.125 * z
            u[r, h + 1, h, 0] = z
            u[r, h + 3, h, 0] = z
            u[r, h + 4, h, 0] = z
    w = layers(rng)
    w[:, :, :8] = 0
    w[:, :, :, :, :, :8] = 0
    for g in range(8): w[:, g, 2, 0, g, 2, 0] = -0.5
    return {"x": x.reshape(N, 128, 4 * C).astype(BF), "u": u.reshape(N, 128, 512), "v": d["v"], "ring": rings(rng), **weights(rng, w)}
def setup_inputs_late(rng):
    d = numbers_of(rng)
    x = d["x"].astype(np.float32).reshape(N, 8, 16, C, 4)
    x[:, :, 0] = ((rng.permutation(N) % 2) * 0.25 - 0.125)[:, None, None, None]
    s = (N, 8, 8, C, 4)
    x[:, :, 8:] = rng.choice([-1.0, 1.0], s) * (1.0 + 0.125 * (2 * rng.integers(0, 4, s) + 1)) * np.exp2(10.0 - rng.integers(8, 15, s))
    x[:, :, 8, :, 0] = rng.choice([-1.0, 1.0], (N, 8, C)) * 1.96875 * 2.0 ** 10
    u = d["u"].reshape(N, 128, 128, 4)
    u[:, :, ::16] = 0
    for h in range(0, 128, 16): u[:, h, h, 0] = 1.0
    w = layers(rng)
    w[:, :, 8] = 0
    w[:, :, :, :, :, 8:] = (w[:, :, :, :, :, 8:].astype(np.float32) * np.float32(0.125)).astype(BF)
    w[:, :, :, 0, :, 8] = 0
    for g in range(8): w[:, g, 8, 0, g, 8, 0] = -0.5
    return {"x": x.reshape(N, 128, 4 * C).astype(BF), "u": u.reshape(N, 128, 512), "v": d["v"], "ring": rings(rng), **weights(rng, w)}
def setup_inputs_ends(rng):
    d = numbers_of(rng)
    o = rng.permutation(N)
    x = np.zeros((N, 8, 16, C, 4), np.float32)
    u = d["u"].reshape(N, 128, 128, 4)
    u[:, :, ::16] = 0
    v = rng.choice([-1.0, 1.0], (N, 128, 512)).astype(np.float32)
    w = np.zeros((N, 8, 16, 4, 8, 16, 4), np.float32)
    for r in range(N):
        i = o[r] % 4
        k = np.array([1.0, 1.0, 1.0, -1.0, -1.0, -1.0, 0.0, 0.0])[rng.permutation(8)]
        x[r, :, :8] = k[:, None, None, None] * (2.0 ** 14 if i % 2 == 0 else 2.0 ** -30)
        x[r, :, 8:] = 2.0 ** 14 * rng.choice([-1.0, 1.0], (1, 1, C, 1) if i < 2 else (8, 8, C, 4))
        z = 2.0 ** 30 if i // 2 == 0 else 2.0 ** -30
        s = rng.choice([-1.0, 1.0])
        for h in range(0, 128, 16): u[r, h:h + 8, h] = s * z
        v[r] *= np.float32(z)
        w[r, :, 8:, :, :, 8:] = 1.96875 if i == 0 else -1.96875 if i == 3 else (1.96875 if i == 1 else 2.0 ** -30) * rng.choice([-1.0, 1.0], (8, 8, 4, 8, 8, 4))
    return {"x": x.reshape(N, 128, 4 * C).astype(BF), "u": u.reshape(N, 128, 512), "v": v.astype(BF), "ring": rings(rng, True), **weights(rng, w.astype(BF))}
def setup_inputs_spread(rng):
    d = setup_inputs(rng)
    d["x"] = big(wide(rng, N, 128, 4 * C, cols=3).astype(np.float32) * np.float32(0.03125))
    return d
def check_inputs(d):
    b = []
    for k, most in (("x", 2.0 ** 14), ("u", 2.0 ** 30), ("v", 2.0 ** 30)):
        a = np.abs(d[k].astype(np.float32))
        if not (np.isfinite(a).all() and ((a == 0) | (a >= 2.0 ** -30) & (a <= most)).all()): b.append("a value of " + k)
    if (d["ring"] != d["ring"][:1]).any(): b.append("ring isn't the same on all ranks")
    e = gentries(d["ring"][0])
    if not ((e >= 0) & (e < 8 * C)).all(): b.append("an entry of ring")
    for g in range(8):
        h = e[g] // C
        if np.unique(e[g]).size != L: b.append("a place twice in a ring")
        if np.count_nonzero(h == g) != C or np.count_nonzero(h == (g - 1) % 8) != B or np.count_nonzero(h == (g + 1) % 8) != B: b.append("the groups of a ring's places")
    for k in range(2):
        if np.unique(e[k::2]).size != 4 * L: b.append("rings of equal parity share a place")
    none, least, most = [emit(mx_ref.quantize(np.full((128, 16), k, np.float32).astype(BF)))[1][0, 0] for k in (0.0, 2.0 ** -30, 1.96875)]
    for r in range(N):
        if ((d["wc"][r] == 0x7F) | (d["wc"][r] == 0xFF)).any(): b.append("wc: a code that is no number")
        s = mx_ref.live(d["ws"][r])
        if ((s != none) & ((s < least) | (s > most))).any(): b.append("ws: a scale out of range")
        elif (np.abs(decode(pk(d["wc"][r], d["ws"][r]))) > 2.0).any(): b.append("a number of W beyond 2 in size")
    return b
def turned(e, a):
    now = np.arange(8 * C)
    for first in (1, 0):
        new = now.copy()
        for g in range(first, 8, 2): new[np.roll(e[g], -a[g])] = now[e[g]]
        now = new
    return now.reshape(8, C)
def reference(x, u, v, ring, wc, ws):
    qu = [mx_ref.quantize(u[r]) for r in range(N)]
    lay = [pk(wc[r], ws[r]) for r in range(N)]
    now = [x[r] for r in range(N)]
    e = gentries(ring[0])
    ac = np.zeros((N, 8, R), np.float32)
    for t in range(R):
        own, sent = [], []
        for r in range(N):
            q = mx_ref.quantize(now[r])
            s = mx_ref.matmul(qu[r], q)
            a = np.count_nonzero(s[::16] > 0, axis=1)
            ac[r, :, t] = a
            p = turned(e, a)
            own.append(np.ascontiguousarray(decode(q).reshape(8, 16, C, 4)[p // C, :, p % C].transpose(0, 2, 1, 3)).reshape(128, 4 * C).astype(BF))
            sent.append(decode(mx_ref.quantize(np.ascontiguousarray(own[r][:, :4 * M]))).astype(BF))
        for r in range(N):
            z = np.concatenate([sent[r ^ MASK[t]], own[r][:, 4 * M:]], axis=1)
            q = mx_ref.quantize(z)
            now[r] = tile([mx_ref.matmul(pick(lay[r], np.arange(128 * b, 128 * b + 128)), q) * np.float32(0.03125) + z[:, b::4].astype(np.float32) for b in range(4)])
    y = np.zeros((N, 128, C), np.float32)
    oc, osc = np.zeros((N, 128, 4 * C), np.uint8), np.zeros((N, 16, C), np.uint8)
    for r in range(N):
        q = mx_ref.quantize(now[r])
        y[r] = mx_ref.matmul(mx_ref.quantize(v[r]), q)
        oc[r], osc[r] = emit(q)
    return {"y": y, "ac": ac, "oc": oc, "osc": osc}

@@ -1,0 +1,394 @@
+from concourse.bass import DstId, RemoteDMATransfer
+from concourse.mybir import dt, AluOpType as A, ActivationFunctionType as F
+
+C, M0, M1 = 288, 128, 160
+ROUNDS = 3
+MASK = [1, 2, 4]
+SB = 160
+BLK = 4 * SB
+W1 = 7 * BLK
+WIN = 14 * BLK
+WLEN = WIN - 3 * SB
+BF, FP, I32, U16, X4, U8 = "bfloat16", "float32", "int32", "uint16", "float8_e4m3fn_x4", "uint8"
+
+SCRATCH = {"ps": ("psum", [128, 4096], FP)}
+
+
+def _buf(n, name, d):
+    SCRATCH[name] = ("sbuf", [128, n], d)
+
+
+for _n, _w in (("xt", 4 * C), ("ut", 512), ("vt", 512), ("X0", 512), ("X1", 640), ("G0", 512), ("Z0", 512), ("Z1", 640), ("za", 512),
+               ("zb", 640), ("it", 512), ("on", 512), ("big", 2180), ("win", WIN)):
+    _buf(_w, _n, BF)
+for _n, _w in (("uq", 128), ("vq", 128), ("xq0", 128), ("xq1", 160), ("zq0", 128), ("zq1", 160), ("iq", 128), ("oq", 128), ("wq", 512),
+               ("cq0", 416), ("cq1", 416), ("cq2", 416), ("cq3", 416), ("eq0", 128), ("eq1", 128), ("eq2", 128), ("eq3", 128),
+               ("gq0", 128), ("gq1", 128), ("gq2", 128), ("lq0", 128), ("lq1", 128), ("lq2", 128)):
+    _buf(_w, _n, X4)
+    _buf(_w, _n + "s", U8)
+for _n, _w in (("rf0", 512), ("rf1", 640), ("RO", 120), ("RE", 120), ("r1", 120), ("rw", 120), ("rel", 120), ("vals", 1152), ("IO", 2016),
+               ("IE", 2016), ("K", 1824), ("E", 4320), ("jj", 384), ("DM", C), ("RST", C), ("RST3", 54), ("RST4", 72), ("mk", C), ("cs", C),
+               ("p1", 18), ("nA", 18), ("nB", 18), ("n2", 18), ("n3", 18), ("TB1", 54), ("sc1", 54), ("TB2", 72), ("sc2", 72), ("cw", 24),
+               ("LB", 24), ("df", 4), ("pc", 8), ("yt", C), ("ca", 24)):
+    _buf(_w, _n, FP)
+for _n, _w in (("R", 144), ("pn", 16), ("own", 18), ("DMi", C), ("DMj", C)):
+    _buf(_w, _n, I32)
+for _n, _w in (("off", 138), ("offL", 2), ("off1", 18), ("off2", 18), ("off3", 18)):
+    _buf(_w, _n, U16)
+
+SEMAPHORES = ["spe", "sve", "sac", "sgp", "ldx", "ldu", "ldr", "ldw", "ldv", "sh0", "sh1", "sh2", "edb", "fin1", "fin0", "finy", "finc",
+              "ra0", "ra1", "ra2", "lsent"]
+
+
+def rank_program(g, core, T, topo):
+    rank = T.rank_of(core)
+    if rank is None:
+        return
+    Q = {"pe": g.tensor, "ve": g.vector, "ac": g.scalar, "gp": g, "sy": g.sync}
+    SEM = {"pe": "spe", "ve": "sve", "ac": "sac", "gp": "sgp"}
+    count = {}
+    known = {q: {} for q in Q}
+    book = {}
+
+    def touch(q, rd, wr):
+        need = []
+        for r, w in [(r, False) for r in rd] + [(r, True) for r in wr]:
+            b, lo, hi, m = (tuple(r) + (15,))[:4]
+            for (l2, h2, m2, w2, q2, tok) in book.get(b, []):
+                if l2 < hi and lo < h2 and m & m2:
+                    if w:
+                        if q2 != q or w2: need.append(tok)
+                    elif w2 or (b == "ps" and q2 != q):
+                        need.append(tok)
+        return need
+
+    def settle(q, need):
+        k = known[q]
+        best = {}
+        for t in need:
+            if k.get(t[0], 0) < t[1] and (t[0] not in best or best[t[0]][1] < t[1]):
+                best[t[0]] = t
+        todo = list(best.values())
+        todo = [t for t in todo if not any(u is not t and u[2].get(t[0], 0) >= t[1] for u in todo)]
+        for t in todo:
+            Q[q].wait_ge(T.sem[t[0]], t[1])
+            k[t[0]] = max(k.get(t[0], 0), t[1])
+            for s, v in t[2].items():
+                k[s] = max(k.get(s, 0), v)
+
+    def note(rd, wr, qtag, tok):
+        for r in rd:
+            b, lo, hi, m = (tuple(r) + (15,))[:4]
+            book.setdefault(b, []).append((lo, hi, m, False, qtag, tok))
+        for r in wr:
+            b, lo, hi, m = (tuple(r) + (15,))[:4]
+            book[b] = [e for e in book.get(b, []) if not (lo <= e[0] and e[1] <= hi and e[2] & m == e[2])]
+            book[b].append((lo, hi, m, True, qtag, tok))
+
+    def run(q, fn, rd, wr):
+        settle(q, touch(q, rd, wr))
+        s = SEM[q]
+        fn(Q[q]).then_inc(T.sem[s], 1)
+        count[s] = count.get(s, 0) + 1
+        snap = dict(known[q])
+        snap[s] = count[s]
+        note(rd, wr, q, (s, count[s], snap))
+
+    groups = {}
+
+    def dma(q, grp, out, in_, rd, wr):
+        settle(q, touch(None, rd, wr))
+        Q[q].dma_start(out, in_).then_inc(T.sem[grp], 16)
+        tok = groups.setdefault(grp, [grp, 0, {}])
+        tok[1] += 16
+        for s, v in known[q].items():
+            tok[2][s] = max(tok[2].get(s, 0), v)
+        count[grp] = tok[1]
+        note(rd, wr, None, tok)
+
+    def ts(out, in0, s1, s2, o0, o1, rd, wr):
+        if o1 is None:
+            run("ve", lambda e: e.tensor_scalar(out, in0, s1, s2, o0), rd, wr)
+        else:
+            run("ve", lambda e: e.tensor_scalar(out, in0, s1, s2, o0, o1), rd, wr)
+
+    def tt(out, a, b, o, rd, wr):
+        run("ve", lambda e: e.tensor_tensor(out, a, b, o), rd, wr)
+
+    def tc(out, in_, rd, wr):
+        run("ve", lambda e: e.tensor_copy(out, in_), rd, wr)
+
+    def ms(b, c, lo, hi, step=1, p0=0, p1=128):
+        run("ve", lambda e: e.memset(T[b][p0:p1, lo:hi:step], c), [], [(b, lo, hi)])
+
+    def act(out, in_, rd, wr, scale=1.0):
+        if scale == 1.0:
+            run("ac", lambda e: e.activation(out, in_, F.Copy), rd, wr)
+        else:
+            run("ac", lambda e: e.activation(out, in_, F.Copy, scale=scale), rd, wr)
+
+    def actb(out, in_, bias, rd, wr):
+        run("ac", lambda e: e.activation(out, in_, F.Identity, bias=float(bias)), rd, wr)
+
+    def quant(q, lo, n, src, slo):
+        run("ve", lambda e: e.quantize_mx(T[q][:, lo:lo + n], T[q + "s"][:, lo:lo + n], T[src][:, slo:slo + 4 * n]),
+            [(src, slo, slo + 4 * n)], [(q, lo, lo + n), (q + "s", lo, lo + n)])
+
+    bank = [0]
+
+    def mm(st, slo, mv, mlo, n):
+        b = bank[0]
+        bank[0] = (b + 1) % 8
+        o = T.ps[:, 512 * b:512 * b + n]
+        run("pe", lambda e: e.matmul_mx(o, T[st][:, slo:slo + 128], T[st + "s"][:, slo:slo + 128], T[mv][:, mlo:mlo + n], T[mv + "s"][:, mlo:mlo + n], True, True),
+            [(st, slo, slo + 128), (st + "s", slo, slo + 128), (mv, mlo, mlo + n), (mv + "s", mlo, mlo + n)], [("ps", 512 * b, 512 * b + 512)])
+        return b
+
+    def pr(b):
+        return ("ps", 512 * b, 512 * b + 512)
+
+    def pv(b, n):
+        return T.ps[:, 512 * b:512 * b + n]
+
+    def diag(src, width, offs, ocols):
+        o0, o1 = ocols
+        n = 16 * (o1 - o0)
+        tt(T.mk[:, 0:n], T[src][:, 0:width].indirect(T[offs][:, o0:o1]), T.DM[:, 0:n], A.mult,
+           [(src, 0, width), (offs, o0, o1), ("DM", 0, n)], [("mk", 0, n)])
+        run("ve", lambda e: e.tensor_tensor_scan(T.cs[:, 0:n], T.RST[:, 0:n], T.mk[:, 0:n], 0.0, A.mult, A.add),
+            [("RST", 0, n), ("mk", 0, n)], [("cs", 0, n)])
+
+    dma("sy", "ldx", T.xt[:, :], T.x[:, :], [], [("xt", 0, 4 * C)])
+    dma("ac", "ldu", T.ut[:, :], T.u[:, :], [], [("ut", 0, 512)])
+    turn = 0
+    for i, s in enumerate((-2, 0, 2, -1, 1, 3)):
+        r = 16 * (s % 8)
+        c0, c1 = 24 * i, 24 * i + 24
+        for lo, hi, so in ((0, 128 - r, r), (128 - r, 128, r - 128)):
+            if lo < hi:
+                dma("sy" if turn % 4 else "ac", "ldr", T.R[lo:hi, c0:c1], T.ring[lo + so:hi + so, :], [], [("R", c0, c1, 1 if lo else 2)])
+                turn += 1
+    dma("sy", "ldw", T.wq[:, 0:512].bitcast(dt.uint8), T.wc[:, :], [], [("wq", 0, 512)])
+    dma("sy", "ldw", T.wqs[:, 0:512], T.ws[:, :], [], [("wqs", 0, 512)])
+    dma("sy", "ldv", T.vt[:, :], T.v[:, :], [], [("vt", 0, 512)])
+
+    ms("big", 0.0, 0, 2180)
+    run("gp", lambda e: e.iota(T.pn[:, 0:1], [[1, 1]], 0, 1), [], [("pn", 0, 1)])
+    run("gp", lambda e: e.iota(T.jj[:, :], [[1, 384]], 0, 0, allow_small_or_imprecise_dtypes=True), [], [("jj", 0, 384)])
+    run("gp", lambda e: e.iota(T.own[:, :], [[16, 18]], 576, 0), [], [("own", 0, 18)])
+
+    def ones(c0, c1, pattern, base):
+        v = T.big[:, 3 + 4 * c0:4 * c1:4]
+        run("gp", lambda e: e.affine_select(v, v, pattern, A.not_equal, 1.0, base, -1), [("big", 4 * c0, 4 * c1)], [("big", 4 * c0, 4 * c1)])
+
+    ones(0, 32, [[0, 2], [1, 16]], 96)
+    ones(32, 160, [[32, 4], [0, 2], [1, 16]], 0)
+    ones(160, 224, [[32, 2], [0, 2], [1, 16]], 0)
+    ones(224, 256, [[0, 2], [1, 16]], 112)
+    ones(256, 384, [[32, 4], [0, 2], [1, 16]], 16)
+    ones(384, 416, [[0, 2], [1, 16]], 16)
+    run("gp", lambda e: e.iota(T.DMi[:, :], [[1, C]], 128, -1), [], [("DMi", 0, C)])
+    ones(416, 544, [[1, 128]], 0)
+
+    def pn(i): return T.pn[:, i:i + 1]
+    def pr_(i): return ("pn", i, i + 1)
+    ts(pn(1), pn(0), 4, 1, A.logical_shift_right, A.bitwise_and, [pr_(0)], [pr_(1)])
+    ts(pn(2), pn(0), 15, None, A.bitwise_and, None, [pr_(0)], [pr_(2)])
+    ts(pn(3), pn(0), 4, 6, A.logical_shift_right, A.bitwise_and, [pr_(0)], [pr_(3)])
+    ms("it", 0.0, 0, 512)
+    ms("on", 0.0, 0, 512)
+    tc(T.pc[:, 0:1], pn(1), [pr_(1)], [("pc", 0, 1)])
+    ts(T.pc[:, 1:2], pn(1), -1.0, 1.0, A.mult, A.add, [pr_(1)], [("pc", 1, 2)])
+    ts(pn(4), pn(3), 6.0, None, A.add, None, [pr_(3)], [pr_(4)])
+    ts(pn(11), pn(1), 288.0, None, A.mult, None, [pr_(1)], [pr_(11)])
+    tt(pn(6), pn(3), pn(2), A.add, [pr_(3), pr_(2)], [pr_(6)])
+    ts(pn(9), pn(2), 5.0, 16.0, A.is_ge, A.mult, [pr_(2)], [pr_(9)])
+    ts(pn(5), pn(4), 7, None, A.bitwise_and, None, [pr_(4)], [pr_(5)])
+    tt(pn(12), pn(11), pn(2), A.add, [pr_(11), pr_(2)], [pr_(12)])
+    ts(pn(7), pn(6), 7.0, None, A.add, None, [pr_(6)], [pr_(7)])
+    ts(T.pc[:, 2:3], pn(5), -288.0, None, A.mult, None, [pr_(5)], [("pc", 2, 3)])
+    tc(T.pc[:, 3:4], pn(12), [pr_(12)], [("pc", 3, 4)])
+    ts(pn(8), pn(7), 7, None, A.bitwise_and, None, [pr_(7)], [pr_(8)])
+    ts(T.off[:, 120:138], T.own[:, :], T.pc[:, 3:4], None, A.add, None, [("own", 0, 18), ("pc", 3, 4)], [("off", 120, 138)])
+    tt(pn(10), pn(8), pn(9), A.add, [pr_(8), pr_(9)], [pr_(10)])
+    tc(T.offL[:, 0:1], pn(10), [pr_(10)], [("offL", 0, 2)])
+    ms("on", 1.0, 0, 512, 4)
+    ms("on", 1.0, 1, 512, 4)
+    ms("on", 1.0, 2, 512, 4, 96, 128)
+    ms("RST", 1.0, 0, C)
+    ms("RST", 0.0, 0, C, 16)
+    ms("RST3", 1.0, 0, 54)
+    ms("RST3", 0.0, 0, 54, 3)
+    ms("RST4", 1.0, 0, 72)
+    ms("RST4", 0.0, 0, 72, 4)
+    ms("cw", 384.0, 0, 24)
+    ms("LB", 384.0, 0, 24)
+
+    for s in range(3):
+        actb(T.vals[:, 384 * s:384 * s + 384], T.jj[:, :], 768 * s, [("jj", 0, 384)], [("vals", 384 * s, 384 * s + 384)])
+    actb(T.IE[:, 864:1152], T.jj[:, 0:C], 1536, [("jj", 0, C)], [("IE", 864, 1152)])
+    for lo in (576, 1152):
+        actb(T.IO[:, lo:lo + C], T.jj[:, 0:C], 2304 + lo, [("jj", 0, C)], [("IO", lo, lo + C)])
+    for D in range(7):
+        lo = 2304 + C * D
+        actb(T.E[:, lo:lo + M0], T.jj[:, 0:M0], BLK * D, [("jj", 0, M0)], [("E", lo, lo + M0)])
+        actb(T.E[:, lo + M0:lo + C], T.jj[:, M0:C], BLK * D + W1 - M0, [("jj", M0, C)], [("E", lo + M0, lo + C)])
+
+    def score(blk):
+        st, lo = (("xq0", 0), ("xq1", 0), ("xq1", 32))[blk]
+        b = mm(st, lo, "uq", 0, 128)
+        ts(T.it[:, blk:32:4], T.ps[:, 512 * b:512 * b + 128:16], 0.0, None, A.is_gt, None, [pr(b)], [("it", 0, 32, 1 << blk)])
+
+    def unpack(D, b, q, n, where, eng="ac"):
+        lo = 32 * (D // 2) + (224 if D % 2 else 0)
+        k = mm("cq%d" % b, lo, q, 0, n)
+        at = where + BLK * D + SB * b
+        if eng == "ac":
+            act(T.win[:, at:at + n], pv(k, n), [pr(k)], [("win", at, at + n)])
+        else:
+            tc(T.win[:, at:at + n], pv(k, n), [pr(k)], [("win", at, at + n)])
+
+    def early(t):
+        score(1)
+        score(2)
+        for D in (2, 3):
+            for b in range(4):
+                unpack(D, b, "xq1", M1, W1)
+        src = W1 + 2 * BLK
+        for k, (dst, n, sh) in enumerate(((0, 2 * BLK, -32), (4 * BLK, 2 * BLK, 32), (6 * BLK, BLK, 64))):
+            s = sh % 128
+            d0 = W1 + dst
+            for lo, hi, so in ((0, 128 - s, s), (128 - s, 128, s - 128)):
+                dma("sy", "sh%d" % t, T.win[lo:hi, d0:d0 + n], T.win[lo + so:hi + so, src:src + n],
+                    [("win", src, src + n)], [("win", d0, d0 + n, 1 if lo else 2)])
+
+    def window():
+        score(0)
+        quant("iq", 0, 128, "it", 0)
+        i = 0
+        for D in (2, 3, 1, 4, 0, 5, 6):
+            for b in range(4):
+                unpack(D, b, "xq0", M0, 0)
+                i += 1
+                if i == 5:
+                    k = mm("oq", 0, "iq", 0, 128)
+                    tc(T.cw[:, 0:8], pv(k, 8), [pr(k)], [("cw", 0, 8)])
+
+    def lists():
+        tc(T.LB[:, 2:18], T.cw[:, 0:24].indirect(T.offL[:, 0:1]), [("cw", 0, 24), ("offL", 0, 2)], [("LB", 2, 18)])
+        ts(T.TB1[:, 1:54:3], T.nA[:, :], T.LB[:, 3:4], None, A.mult, None, [("nA", 0, 18), ("LB", 3, 4)], [("TB1", 0, 54, 2)])
+        ts(T.TB1[:, 2:54:3], T.nB[:, :], T.LB[:, 5:6], None, A.mult, None, [("nB", 0, 18), ("LB", 5, 6)], [("TB1", 0, 54, 4)])
+        tt(T.df[:, :], T.LB[:, 0:8:2], T.LB[:, 2:10:2], A.subtract, [("LB", 0, 10)], [("df", 0, 4)])
+        run("ve", lambda e: e.tensor_tensor_scan(T.sc1[:, :], T.RST3[:, :], T.TB1[:, :], 0.0, A.mult, A.add), [("RST3", 0, 54), ("TB1", 0, 54)], [("sc1", 0, 54)])
+        tc(T.off1[:, :], T.sc1[:, 2:54:3], [("sc1", 0, 54)], [("off1", 0, 18)])
+        diag("K", 1824, "off1", (0, 18))
+        z = T.cs[:, 15:C:16]
+        ts(T.TB2[:, 0:72:4], z, T.df[:, 0:1], None, A.add, None, [("cs", 0, C), ("df", 0, 1)], [("TB2", 0, 72, 1)])
+        for i in (1, 2, 3):
+            ts(T.TB2[:, i:72:4], z, 768.0 * i, T.df[:, i:i + 1], A.is_ge, A.mult, [("cs", 0, C), ("df", i, i + 1)], [("TB2", 0, 72, 1 << i)])
+        run("ve", lambda e: e.tensor_tensor_scan(T.sc2[:, :], T.RST4[:, :], T.TB2[:, :], 0.0, A.mult, A.add), [("RST4", 0, 72), ("TB2", 0, 72)], [("sc2", 0, 72)])
+        tc(T.off2[:, :], T.sc2[:, 3:72:4], [("sc2", 0, 72)], [("off2", 0, 18)])
+        diag("E", 4320, "off2", (0, 18))
+        tc(T.off3[:, :], T.cs[:, 15:C:16], [("cs", 0, C)], [("off3", 0, 18)])
+
+    def gather(dst, n, o0, o1):
+        for b in (0, 2, 1, 3):
+            o = T[dst][:, b:4 * n:4]
+            i = T.win[:, SB * b:SB * b + WLEN].indirect(T.off3[:, o0:o1])
+            (tc if b < 2 else act)(o, i, [("win", SB * b, SB * b + WLEN), ("off3", o0, o1)], [(dst, 0, 4 * n, 1 << b)])
+
+    def layer(zq, n, z32, rf, X):
+        for b in range(4):
+            k = mm("wq", 128 * b, zq, 0, n)
+            lo = n * b
+            tt(T[rf][:, lo:lo + n], pv(k, n), T[z32][:, b:4 * n:4], A.add, [pr(k), (z32, 0, 4 * n)], [(rf, lo, lo + n)])
+            act(T[X][:, b:4 * n:4], T[rf][:, lo:lo + n], [(rf, lo, lo + n)], [(X, 0, 4 * n, 1 << b)], scale=0.03125)
+
+    def times32(dst, src, n):
+        ts(T[dst][:, 0:n], T[src][:, 0:n], 32.0, None, A.mult, None, [(src, 0, n)], [(dst, 0, n)])
+
+    quant("oq", 0, 128, "on", 0)
+    quant("uq", 0, 128, "ut", 0)
+    quant("xq1", 0, M1, "xt", 512)
+    quant("xq0", 0, M0, "xt", 0)
+    for b in range(4):
+        quant("cq%d" % b, 0, 416, "big", 3 - b)
+    ts(T.RO[:, :], T.R[:, 0:120], T.pc[:, 0:1], T.pc[:, 2:3], A.mult, A.add, [("R", 0, 120), ("pc", 0, 3)], [("RO", 0, 120)])
+    ts(T.RE[:, 0:72], T.R[:, 72:144], T.pc[:, 1:2], None, A.mult, None, [("R", 72, 144), ("pc", 1, 2)], [("RE", 0, 72)])
+    ts(T.RE[:, 72:120], T.R[:, 24:72], T.pc[:, 1:2], None, A.mult, None, [("R", 24, 72), ("pc", 1, 2)], [("RE", 72, 120)])
+    tt(T.r1[:, :], T.RO[:, :], T.RE[:, :], A.add, [("RO", 0, 120), ("RE", 0, 120)], [("r1", 0, 120)])
+    ts(T.rw[:, :], T.r1[:, :], 0.0, 2304.0, A.is_lt, A.mult, [("r1", 0, 120)], [("rw", 0, 120)])
+    tt(T.rel[:, :], T.r1[:, :], T.rw[:, :], A.add, [("r1", 0, 120), ("rw", 0, 120)], [("rel", 0, 120)])
+    tc(T.off[:, 0:120], T.rel[:, :], [("rel", 0, 120)], [("off", 0, 120)])
+    tc(T.IO[:, 0:2016].indirect(T.off[:, 0:72]), T.vals[:, :], [("off", 0, 72), ("vals", 0, 1152)], [("IO", 0, 2016)])
+    early(0)
+    for s in range(3):
+        lo = 768 * s
+        act(T.E[:, lo:lo + 384], T.E[:, 2304:4320].indirect(T.off[:, 24 * s:24 * s + 24]), [("E", 2304, 4320), ("off", 24 * s, 24 * s + 24)], [("E", lo, lo + 384)])
+        dma("sy", "edb", T.E[:, lo + 384:lo + 768], T.E[:, lo:lo + 384], [("E", lo, lo + 384)], [("E", lo + 384, lo + 768)])
+    for lo, o0, n in ((0, 72, 24), (768, 96, 24), (1536, 120, 18)):
+        act(T.K[:, lo:lo + 16 * n], T.IO[:, 0:2016].indirect(T.off[:, o0:o0 + n]), [("IO", 0, 2016), ("off", o0, o0 + n)], [("K", lo, lo + 16 * n)])
+    tc(T.IE[:, 0:2016].indirect(T.off[:, 72:120]), T.vals[:, 0:768], [("off", 72, 120), ("vals", 0, 768)], [("IE", 0, 2016)])
+    ts(T.DMj[:, :], T.DMi[:, :], 15, None, A.bitwise_and, None, [("DMi", 0, C)], [("DMj", 0, C)])
+    ts(T.DM[:, :], T.DMj[:, :], 0.0, None, A.is_equal, None, [("DMj", 0, C)], [("DM", 0, C)])
+    diag("IE", 2016, "off", (120, 138))
+    tc(T.p1[:, :], T.cs[:, 15:C:16], [("cs", 0, C)], [("p1", 0, 18)])
+    ts(T.nA[:, :], T.p1[:, :], 768.0, -1.0, A.is_lt, A.mult, [("p1", 0, 18)], [("nA", 0, 18)])
+    ts(T.n2[:, :], T.p1[:, :], 1536.0, -1.0, A.is_lt, A.mult, [("p1", 0, 18)], [("n2", 0, 18)])
+    tt(T.nB[:, :], T.n2[:, :], T.nA[:, :], A.subtract, [("n2", 0, 18), ("nA", 0, 18)], [("nB", 0, 18)])
+    ts(T.n3[:, :], T.n2[:, :], -384.0, None, A.mult, None, [("n2", 0, 18)], [("n3", 0, 18)])
+    tt(T.TB1[:, 0:54:3], T.p1[:, :], T.n3[:, :], A.add, [("p1", 0, 18), ("n3", 0, 18)], [("TB1", 0, 54, 1)])
+    for lo in (0, 768):
+        tc(T.K[:, lo + 384:lo + 768], T.K[:, lo:lo + 384], [("K", lo, lo + 384)], [("K", lo + 384, lo + 768)])
+
+    for t in range(ROUNDS):
+        last = t == ROUNDS - 1
+        window()
+        lists()
+        gather("G0", M0, 0, 8)
+        gq, lq = "gq%d" % t, "lq%d" % t
+        quant(gq, 0, M0, "G0", 0)
+        dst = T.cores[rank ^ MASK[t]]
+        rid, pid = topo.addr(dst, core)
+        mask, ne = topo.mask(core, dst), len(topo.engines(core, dst))
+        settle("gp", touch("gp", [(gq, 0, M0), (gq + "s", 0, M0)], []))
+        for o, i in ((T[lq][:, 0:M0].bitcast(dt.uint8), T[gq][:, 0:M0].bitcast(dt.uint8)), (T[lq + "s"][:, 0:M0], T[gq + "s"][:, 0:M0])):
+            g.remote_dma(out_ap=o, in_ap=i, remote_sem=T.sem["ra%d" % t], local_sem=T.sem.lsent, pid=pid, routing_id=rid, dma_engine_mask=mask)
+        count["ra%d" % t] = 2 * ne
+        count["lsent"] = count.get("lsent", 0) + 2 * ne
+        note([], [(lq, 0, M0), (lq + "s", 0, M0)], None, ("ra%d" % t, 2 * ne, {}))
+        gather("Z1", M1, 8, 18)
+        quant("zq1", 0, M1, "Z1", 0)
+        times32("zb", "Z1", 640)
+        layer("zq1", M1, "zb", "rf1", "X1")
+        quant("xq1", 0, M1, "X1", 0)
+        act(T.ca[:, t:24:3], T.cw[:, 0:8], [("cw", 0, 8)], [("ca", 0, 24)])
+        if t == 0:
+            for b in range(4):
+                quant("eq%d" % b, 0, 128, "big", 3 - b + 1664)
+        if last:
+            dma("sy", "finc", T.ac[:, :], T.ca[0:1, :], [("ca", 0, 24)], [])
+            quant("vq", 0, 128, "vt", 0)
+            dma("sy", "fin1", T.oc[:, 512:1152], T.xq1[:, :].bitcast(dt.uint8), [("xq1", 0, M1)], [])
+            for k in range(4):
+                dma("sy", "fin1", T.osc[4 * k:4 * k + 4, M0:C], T.xq1s[32 * k:32 * k + 4, :], [("xq1s", 0, M1)], [])
+            k = mm("vq", 0, "xq1", 0, M1)
+            act(T.yt[:, M0:C], pv(k, M1), [pr(k)], [("yt", M0, C)])
+            dma("sy", "fin1", T.y[:, M0:C], T.yt[:, M0:C], [("yt", M0, C)], [])
+        else:
+            early(t + 1)
+        for b in range(4):
+            k = mm("eq%d" % b, 0, lq, 0, M0)
+            (tc if b % 2 == 0 else act)(T.Z0[:, b:512:4], pv(k, M0), [pr(k)], [("Z0", 0, 512, 1 << b)])
+        quant("zq0", 0, M0, "Z0", 0)
+        times32("za", "Z0", 512)
+        layer("zq0", M0, "za", "rf0", "X0")
+        quant("xq0", 0, M0, "X0", 0)
+    dma("sy", "fin0", T.oc[:, 0:512], T.xq0[:, :].bitcast(dt.uint8), [("xq0", 0, M0)], [])
+    for k in range(4):
+        dma("sy", "fin0", T.osc[4 * k:4 * k + 4, 0:M0], T.xq0s[32 * k:32 * k + 4, :], [("xq0s", 0, M0)], [])
+    k = mm("vq", 0, "xq0", 0, M0)
+    act(T.yt[:, 0:M0], pv(k, M0), [pr(k)], [("yt", 0, M0)])
+    dma("ac", "finy", T.y[:, 0:M0], T.yt[:, 0:M0], [("yt", 0, M0)], [])
+    for s, v in count.items():
+        g.wait_ge(T.sem[s], v)

@@ -1,4 +1,3 @@
-from concourse.bass import DstId, RemoteDMATransfer
 from concourse.mybir import dt, AluOpType as A, ActivationFunctionType as F
 
 C, M0, M1 = 288, 128, 160
@@ -19,25 +18,25 @@ def _buf(n, name, d):
 
 
 for _n, _w in (("xt", 4 * C), ("ut", 512), ("vt", 512), ("X0", 512), ("X1", 640), ("G0", 512), ("Z0", 512), ("Z1", 640), ("za", 512),
-               ("zb", 640), ("it", 512), ("on", 512), ("big", 2180), ("win", WIN)):
+               ("zb", 640), ("it", 512), ("on", 512), ("big", 2184), ("win", WIN)):
     _buf(_w, _n, BF)
 for _n, _w in (("uq", 128), ("vq", 128), ("xq0", 128), ("xq1", 160), ("zq0", 128), ("zq1", 160), ("iq", 128), ("oq", 128), ("wq", 512),
                ("cq0", 416), ("cq1", 416), ("cq2", 416), ("cq3", 416), ("eq0", 128), ("eq1", 128), ("eq2", 128), ("eq3", 128),
                ("gq0", 128), ("gq1", 128), ("gq2", 128), ("lq0", 128), ("lq1", 128), ("lq2", 128)):
     _buf(_w, _n, X4)
     _buf(_w, _n + "s", U8)
-for _n, _w in (("rf0", 512), ("rf1", 640), ("RO", 120), ("RE", 120), ("r1", 120), ("rw", 120), ("rel", 120), ("vals", 1152), ("IO", 2016),
-               ("IE", 2016), ("K", 1824), ("E", 4320), ("jj", 384), ("DM", C), ("RST", C), ("RST3", 54), ("RST4", 72), ("mk", C), ("cs", C),
-               ("p1", 18), ("nA", 18), ("nB", 18), ("n2", 18), ("n3", 18), ("TB1", 54), ("sc1", 54), ("TB2", 72), ("sc2", 72), ("cw", 24),
-               ("LB", 24), ("df", 4), ("pc", 8), ("yt", C), ("ca", 24)):
+for _n, _w in (("rf0", 512), ("rf1", 640), ("RO", 120), ("RE", 120), ("rel", 120), ("vals", 1152), ("IO", 2304), ("IE", 2304), ("K", 1824),
+               ("E", 4608), ("jj", 384), ("DM", C), ("RST", C), ("RST3", 54), ("RST4", 72), ("mk", C), ("cs", C), ("nA", 18), ("nB", 18),
+               ("n2", 18), ("TB1", 54), ("sc1", 54), ("TB2", 72), ("sc2", 72), ("cw", 24), ("LB", 24), ("df", 4), ("pc", 4), ("sA", 8), ("sB", 8),
+               ("yt", C), ("ca", 24)):
     _buf(_w, _n, FP)
-for _n, _w in (("R", 144), ("pn", 16), ("own", 18), ("DMi", C), ("DMj", C)):
+for _n, _w in (("R", 144), ("pn", 12), ("own", 18), ("hh", 8), ("h2", 8), ("h3", 8), ("DMi", 16), ("DMj", 16)):
     _buf(_w, _n, I32)
 for _n, _w in (("off", 138), ("offL", 2), ("off1", 18), ("off2", 18), ("off3", 18)):
     _buf(_w, _n, U16)
 
-SEMAPHORES = ["spe", "sve", "sac", "sgp", "ldx", "ldu", "ldr", "ldw", "ldv", "sh0", "sh1", "sh2", "edb", "fin1", "fin0", "finy", "finc",
-              "ra0", "ra1", "ra2", "lsent"]
+SEMAPHORES = ["spe", "sve", "sac", "sgp", "ldx", "ldu", "ldr", "ldw", "ldv", "sh0", "sh1", "sh2", "sw0", "sw1", "sw2", "fin1", "fin0", "finy",
+              "finc", "ra0", "ra1", "ra2", "lsent"]
 
 
 def rank_program(g, core, T, topo):
@@ -128,7 +127,7 @@ def rank_program(g, core, T, topo):
             run("ac", lambda e: e.activation(out, in_, F.Copy, scale=scale), rd, wr)
 
     def actb(out, in_, bias, rd, wr):
-        run("ac", lambda e: e.activation(out, in_, F.Identity, bias=float(bias)), rd, wr)
+        run("ac", lambda e: e.activation(out, in_, F.Identity, bias=bias), rd, wr)
 
     def quant(q, lo, n, src, slo):
         run("ve", lambda e: e.quantize_mx(T[q][:, lo:lo + n], T[q + "s"][:, lo:lo + n], T[src][:, slo:slo + 4 * n]),
@@ -159,7 +158,6 @@ def rank_program(g, core, T, topo):
             [("RST", 0, n), ("mk", 0, n)], [("cs", 0, n)])
 
     dma("sy", "ldx", T.xt[:, :], T.x[:, :], [], [("xt", 0, 4 * C)])
-    dma("ac", "ldu", T.ut[:, :], T.u[:, :], [], [("ut", 0, 512)])
     turn = 0
     for i, s in enumerate((-2, 0, 2, -1, 1, 3)):
         r = 16 * (s % 8)
@@ -168,14 +166,17 @@ def rank_program(g, core, T, topo):
             if lo < hi:
                 dma("sy" if turn % 4 else "ac", "ldr", T.R[lo:hi, c0:c1], T.ring[lo + so:hi + so, :], [], [("R", c0, c1, 1 if lo else 2)])
                 turn += 1
+    dma("sy", "ldu", T.ut[:, :], T.u[:, :], [], [("ut", 0, 512)])
     dma("sy", "ldw", T.wq[:, 0:512].bitcast(dt.uint8), T.wc[:, :], [], [("wq", 0, 512)])
     dma("sy", "ldw", T.wqs[:, 0:512], T.ws[:, :], [], [("wqs", 0, 512)])
     dma("sy", "ldv", T.vt[:, :], T.v[:, :], [], [("vt", 0, 512)])
 
-    ms("big", 0.0, 0, 2180)
+    ms("big", 0.0, 0, 2184)
     run("gp", lambda e: e.iota(T.pn[:, 0:1], [[1, 1]], 0, 1), [], [("pn", 0, 1)])
+    run("gp", lambda e: e.iota(T.DMi[:, :], [[1, 16]], 128, -1), [], [("DMi", 0, 16)])
     run("gp", lambda e: e.iota(T.jj[:, :], [[1, 384]], 0, 0, allow_small_or_imprecise_dtypes=True), [], [("jj", 0, 384)])
-    run("gp", lambda e: e.iota(T.own[:, :], [[16, 18]], 576, 0), [], [("own", 0, 18)])
+    run("gp", lambda e: e.iota(T.own[:, :], [[16, 18]], 0, 0), [], [("own", 0, 18)])
+    run("gp", lambda e: e.iota(T.hh[:, :], [[1, 8]], 10, 0), [], [("hh", 0, 8)])
 
     def ones(c0, c1, pattern, base):
         v = T.big[:, 3 + 4 * c0:4 * c1:4]
@@ -187,92 +188,112 @@ def rank_program(g, core, T, topo):
     ones(224, 256, [[0, 2], [1, 16]], 112)
     ones(256, 384, [[32, 4], [0, 2], [1, 16]], 16)
     ones(384, 416, [[0, 2], [1, 16]], 16)
-    run("gp", lambda e: e.iota(T.DMi[:, :], [[1, C]], 128, -1), [], [("DMi", 0, C)])
-    ones(416, 544, [[1, 128]], 0)
+
+    def count_up(b, lo, base):
+        run("gp", lambda e: e.iota(T[b][:, lo:lo + C], [[1, C]], base, 0, allow_small_or_imprecise_dtypes=True), [], [(b, lo, lo + C)])
+
+    for h in (0, 2, 4, 6):
+        count_up("IO", C * h, 2304 + C * h)
+    for h in (1, 3, 5, 7):
+        count_up("IE", C * h, 1536)
+    ones(417, 545, [[1, 128]], 0)
 
     def pn(i): return T.pn[:, i:i + 1]
     def pr_(i): return ("pn", i, i + 1)
+    ts(T.DMj[:, :], T.DMi[:, :], 15, None, A.bitwise_and, None, [("DMi", 0, 16)], [("DMj", 0, 16)])
     ts(pn(1), pn(0), 4, 1, A.logical_shift_right, A.bitwise_and, [pr_(0)], [pr_(1)])
+    ts(T.DM[:, 0:16], T.DMj[:, :], 0.0, None, A.is_equal, None, [("DMj", 0, 16)], [("DM", 0, 16)])
     ts(pn(2), pn(0), 15, None, A.bitwise_and, None, [pr_(0)], [pr_(2)])
     ts(pn(3), pn(0), 4, 6, A.logical_shift_right, A.bitwise_and, [pr_(0)], [pr_(3)])
-    ms("it", 0.0, 0, 512)
-    ms("on", 0.0, 0, 512)
+    ts(pn(4), pn(0), 4, None, A.logical_shift_right, None, [pr_(0)], [pr_(4)])
     tc(T.pc[:, 0:1], pn(1), [pr_(1)], [("pc", 0, 1)])
     ts(T.pc[:, 1:2], pn(1), -1.0, 1.0, A.mult, A.add, [pr_(1)], [("pc", 1, 2)])
-    ts(pn(4), pn(3), 6.0, None, A.add, None, [pr_(3)], [pr_(4)])
-    ts(pn(11), pn(1), 288.0, None, A.mult, None, [pr_(1)], [pr_(11)])
-    tt(pn(6), pn(3), pn(2), A.add, [pr_(3), pr_(2)], [pr_(6)])
-    ts(pn(9), pn(2), 5.0, 16.0, A.is_ge, A.mult, [pr_(2)], [pr_(9)])
-    ts(pn(5), pn(4), 7, None, A.bitwise_and, None, [pr_(4)], [pr_(5)])
-    tt(pn(12), pn(11), pn(2), A.add, [pr_(11), pr_(2)], [pr_(12)])
-    ts(pn(7), pn(6), 7.0, None, A.add, None, [pr_(6)], [pr_(7)])
-    ts(T.pc[:, 2:3], pn(5), -288.0, None, A.mult, None, [pr_(5)], [("pc", 2, 3)])
-    tc(T.pc[:, 3:4], pn(12), [pr_(12)], [("pc", 3, 4)])
-    ts(pn(8), pn(7), 7, None, A.bitwise_and, None, [pr_(7)], [pr_(8)])
+    ts(T.pc[:, 2:3], pn(3), -1.0, None, A.mult, None, [pr_(3)], [("pc", 2, 3)])
+    ts(pn(5), pn(4), 288.0, None, A.mult, None, [pr_(4)], [pr_(5)])
+    tt(pn(7), pn(3), pn(2), A.add, [pr_(3), pr_(2)], [pr_(7)])
+    ts(pn(10), pn(2), 5.0, 16.0, A.is_ge, A.mult, [pr_(2)], [pr_(10)])
+    ts(T.h2[:, :], T.hh[:, :], T.pc[:, 2:3], None, A.add, None, [("hh", 0, 8), ("pc", 2, 3)], [("h2", 0, 8)])
+    tt(pn(6), pn(5), pn(2), A.add, [pr_(5), pr_(2)], [pr_(6)])
+    ts(pn(8), pn(7), 7.0, None, A.add, None, [pr_(7)], [pr_(8)])
+    ts(T.h3[:, :], T.h2[:, :], 7, None, A.bitwise_and, None, [("h2", 0, 8)], [("h3", 0, 8)])
+    tc(T.pc[:, 3:4], pn(6), [pr_(6)], [("pc", 3, 4)])
+    ts(pn(9), pn(8), 7, None, A.bitwise_and, None, [pr_(8)], [pr_(9)])
+    ts(T.sA[:, :], T.h3[:, :], float(BLK), None, A.mult, None, [("h3", 0, 8)], [("sA", 0, 8)])
+    ts(T.sB[:, :], T.h3[:, :], float(BLK), float(W1 - M0), A.mult, A.add, [("h3", 0, 8)], [("sB", 0, 8)])
     ts(T.off[:, 120:138], T.own[:, :], T.pc[:, 3:4], None, A.add, None, [("own", 0, 18), ("pc", 3, 4)], [("off", 120, 138)])
-    tt(pn(10), pn(8), pn(9), A.add, [pr_(8), pr_(9)], [pr_(10)])
-    tc(T.offL[:, 0:1], pn(10), [pr_(10)], [("offL", 0, 2)])
-    ms("on", 1.0, 0, 512, 4)
-    ms("on", 1.0, 1, 512, 4)
-    ms("on", 1.0, 2, 512, 4, 96, 128)
-    ms("RST", 1.0, 0, C)
-    ms("RST", 0.0, 0, C, 16)
+    tt(pn(11), pn(9), pn(10), A.add, [pr_(9), pr_(10)], [pr_(11)])
     ms("RST3", 1.0, 0, 54)
-    ms("RST3", 0.0, 0, 54, 3)
+    tc(T.offL[:, 0:1], pn(11), [pr_(11)], [("offL", 0, 2)])
     ms("RST4", 1.0, 0, 72)
+    ms("RST3", 0.0, 0, 54, 3)
     ms("RST4", 0.0, 0, 72, 4)
-    ms("cw", 384.0, 0, 24)
-    ms("LB", 384.0, 0, 24)
+    ms("cw", 0.0, 0, 24)
+    ms("LB", 0.0, 0, 24)
 
+    def fill(b, lo, hi, c):
+        for k in range(lo, hi, 384):
+            n = min(384, hi - k)
+            run("ac", lambda e: e.activation(T[b][:, k:k + n], T.jj[:, 0:n], F.Identity, bias=c, scale=0.0), [("jj", 0, n)], [(b, k, k + n)])
+
+    fill("on", 0, 512, 1.0)
+    run("ac", lambda e: e.activation(T.RST[:, 0:16], T.jj[:, 0:16], F.Sign), [("jj", 0, 16)], [("RST", 0, 16)])
+    fill("it", 0, 512, 0.0)
+    for lo, n in ((16, 16), (32, 32), (64, 64), (128, 128), (256, 32)):
+        for b in ("DM", "RST"):
+            act(T[b][:, lo:lo + n], T[b][:, 0:n], [(b, 0, n)], [(b, lo, lo + n)])
     for s in range(3):
-        actb(T.vals[:, 384 * s:384 * s + 384], T.jj[:, :], 768 * s, [("jj", 0, 384)], [("vals", 384 * s, 384 * s + 384)])
-    actb(T.IE[:, 864:1152], T.jj[:, 0:C], 1536, [("jj", 0, C)], [("IE", 864, 1152)])
-    for lo in (576, 1152):
-        actb(T.IO[:, lo:lo + C], T.jj[:, 0:C], 2304 + lo, [("jj", 0, C)], [("IO", lo, lo + C)])
-    for D in range(7):
-        lo = 2304 + C * D
-        actb(T.E[:, lo:lo + M0], T.jj[:, 0:M0], BLK * D, [("jj", 0, M0)], [("E", lo, lo + M0)])
-        actb(T.E[:, lo + M0:lo + C], T.jj[:, M0:C], BLK * D + W1 - M0, [("jj", M0, C)], [("E", lo + M0, lo + C)])
+        actb(T.vals[:, 384 * s:384 * s + 384], T.jj[:, :], 768.0 * s, [("jj", 0, 384)], [("vals", 384 * s, 384 * s + 384)])
+    fill("win", 2 * BLK, 3 * BLK, 0.0)
+    for h in range(8):
+        lo = 2304 + C * h
+        actb(T.E[:, lo:lo + M0], T.jj[:, 0:M0], T.sA[:, h:h + 1], [("jj", 0, M0), ("sA", h, h + 1)], [("E", lo, lo + M0)])
+        actb(T.E[:, lo + M0:lo + C], T.jj[:, M0:C], T.sB[:, h:h + 1], [("jj", M0, C), ("sB", h, h + 1)], [("E", lo + M0, lo + C)])
 
     def score(blk):
         st, lo = (("xq0", 0), ("xq1", 0), ("xq1", 32))[blk]
         b = mm(st, lo, "uq", 0, 128)
         ts(T.it[:, blk:32:4], T.ps[:, 512 * b:512 * b + 128:16], 0.0, None, A.is_gt, None, [pr(b)], [("it", 0, 32, 1 << blk)])
 
-    def unpack(D, b, q, n, where, eng="ac"):
+    def unpack(D, b, q, n, where):
         lo = 32 * (D // 2) + (224 if D % 2 else 0)
         k = mm("cq%d" % b, lo, q, 0, n)
         at = where + BLK * D + SB * b
-        if eng == "ac":
-            act(T.win[:, at:at + n], pv(k, n), [pr(k)], [("win", at, at + n)])
-        else:
-            tc(T.win[:, at:at + n], pv(k, n), [pr(k)], [("win", at, at + n)])
+        act(T.win[:, at:at + n], pv(k, n), [pr(k)], [("win", at, at + n)])
+
+    def spread(sem, base, blocks):
+        src = base + 2 * BLK
+        for dst, n, sh in blocks:
+            r = sh % 128
+            d0 = base + dst
+            for lo, hi, so in ((0, 128 - r, r), (128 - r, 128, r - 128)):
+                dma("sy", sem, T.win[lo:hi, d0:d0 + n], T.win[lo + so:hi + so, src:src + n],
+                    [("win", src, src + n)], [("win", d0, d0 + n, 1 if lo else 2)])
 
     def early(t):
-        score(1)
-        score(2)
         for D in (2, 3):
             for b in range(4):
                 unpack(D, b, "xq1", M1, W1)
-        src = W1 + 2 * BLK
-        for k, (dst, n, sh) in enumerate(((0, 2 * BLK, -32), (4 * BLK, 2 * BLK, 32), (6 * BLK, BLK, 64))):
-            s = sh % 128
-            d0 = W1 + dst
-            for lo, hi, so in ((0, 128 - s, s), (128 - s, 128, s - 128)):
-                dma("sy", "sh%d" % t, T.win[lo:hi, d0:d0 + n], T.win[lo + so:hi + so, src:src + n],
-                    [("win", src, src + n)], [("win", d0, d0 + n, 1 if lo else 2)])
+        spread("sh%d" % t, W1, ((0, 2 * BLK, -32), (4 * BLK, 2 * BLK, 32), (6 * BLK, BLK, 64)))
 
-    def window():
-        score(0)
-        quant("iq", 0, 128, "it", 0)
+    def add_up():
+        k = mm("oq", 0, "iq", 0, 128)
+        ts(T.cw[:, 0:8], pv(k, 8), -384.0, None, A.add, None, [pr(k)], [("cw", 0, 8)])
+
+    def window(t):
+        if t:
+            score(0)
+            quant("iq", 0, 128, "it", 0)
         i = 0
-        for D in (2, 3, 1, 4, 0, 5, 6):
+        for D in (2, 3, 1, 4, 5, 6):
             for b in range(4):
                 unpack(D, b, "xq0", M0, 0)
                 i += 1
-                if i == 5:
-                    k = mm("oq", 0, "iq", 0, 128)
-                    tc(T.cw[:, 0:8], pv(k, 8), [pr(k)], [("cw", 0, 8)])
+                if i == (2 if t else 8):
+                    add_up()
+            if D == 2:
+                spread("sw%d" % t, 0, ((0, BLK, -32),))
+                if t == 0:
+                    table_e()
 
     def lists():
         tc(T.LB[:, 2:18], T.cw[:, 0:24].indirect(T.offL[:, 0:1]), [("cw", 0, 24), ("offL", 0, 2)], [("LB", 2, 18)])
@@ -288,7 +309,7 @@ def rank_program(g, core, T, topo):
             ts(T.TB2[:, i:72:4], z, 768.0 * i, T.df[:, i:i + 1], A.is_ge, A.mult, [("cs", 0, C), ("df", i, i + 1)], [("TB2", 0, 72, 1 << i)])
         run("ve", lambda e: e.tensor_tensor_scan(T.sc2[:, :], T.RST4[:, :], T.TB2[:, :], 0.0, A.mult, A.add), [("RST4", 0, 72), ("TB2", 0, 72)], [("sc2", 0, 72)])
         tc(T.off2[:, :], T.sc2[:, 3:72:4], [("sc2", 0, 72)], [("off2", 0, 18)])
-        diag("E", 4320, "off2", (0, 18))
+        diag("E", 4608, "off2", (0, 18))
         tc(T.off3[:, :], T.cs[:, 15:C:16], [("cs", 0, C)], [("off3", 0, 18)])
 
     def gather(dst, n, o0, o1):
@@ -307,43 +328,52 @@ def rank_program(g, core, T, topo):
     def times32(dst, src, n):
         ts(T[dst][:, 0:n], T[src][:, 0:n], 32.0, None, A.mult, None, [(src, 0, n)], [(dst, 0, n)])
 
+    ms("on", 0.0, 2, 512, 4, 0, 96)
     quant("oq", 0, 128, "on", 0)
-    quant("uq", 0, 128, "ut", 0)
+    quant("cq0", 0, 416, "big", 3)
+    quant("cq1", 0, 416, "big", 2)
     quant("xq1", 0, M1, "xt", 512)
     quant("xq0", 0, M0, "xt", 0)
-    for b in range(4):
-        quant("cq%d" % b, 0, 416, "big", 3 - b)
-    ts(T.RO[:, :], T.R[:, 0:120], T.pc[:, 0:1], T.pc[:, 2:3], A.mult, A.add, [("R", 0, 120), ("pc", 0, 3)], [("RO", 0, 120)])
+    quant("cq2", 0, 416, "big", 1)
+    quant("cq3", 0, 416, "big", 0)
+    early(0)
+    ts(T.RO[:, :], T.R[:, 0:120], T.pc[:, 0:1], None, A.mult, None, [("R", 0, 120), ("pc", 0, 1)], [("RO", 0, 120)])
     ts(T.RE[:, 0:72], T.R[:, 72:144], T.pc[:, 1:2], None, A.mult, None, [("R", 72, 144), ("pc", 1, 2)], [("RE", 0, 72)])
     ts(T.RE[:, 72:120], T.R[:, 24:72], T.pc[:, 1:2], None, A.mult, None, [("R", 24, 72), ("pc", 1, 2)], [("RE", 72, 120)])
-    tt(T.r1[:, :], T.RO[:, :], T.RE[:, :], A.add, [("RO", 0, 120), ("RE", 0, 120)], [("r1", 0, 120)])
-    ts(T.rw[:, :], T.r1[:, :], 0.0, 2304.0, A.is_lt, A.mult, [("r1", 0, 120)], [("rw", 0, 120)])
-    tt(T.rel[:, :], T.r1[:, :], T.rw[:, :], A.add, [("r1", 0, 120), ("rw", 0, 120)], [("rel", 0, 120)])
+    tt(T.rel[:, :], T.RO[:, :], T.RE[:, :], A.add, [("RO", 0, 120), ("RE", 0, 120)], [("rel", 0, 120)])
     tc(T.off[:, 0:120], T.rel[:, :], [("rel", 0, 120)], [("off", 0, 120)])
-    tc(T.IO[:, 0:2016].indirect(T.off[:, 0:72]), T.vals[:, :], [("off", 0, 72), ("vals", 0, 1152)], [("IO", 0, 2016)])
-    early(0)
+    quant("uq", 0, 128, "ut", 0)
+    tc(T.IO[:, 0:2304].indirect(T.off[:, 0:72]), T.vals[:, :], [("off", 0, 72), ("vals", 0, 1152)], [("IO", 0, 2304)])
+    for k in (1, 2, 0):
+        score(k)
+    quant("iq", 0, 128, "it", 0)
     for s in range(3):
         lo = 768 * s
-        act(T.E[:, lo:lo + 384], T.E[:, 2304:4320].indirect(T.off[:, 24 * s:24 * s + 24]), [("E", 2304, 4320), ("off", 24 * s, 24 * s + 24)], [("E", lo, lo + 384)])
-        dma("sy", "edb", T.E[:, lo + 384:lo + 768], T.E[:, lo:lo + 384], [("E", lo, lo + 384)], [("E", lo + 384, lo + 768)])
-    for lo, o0, n in ((0, 72, 24), (768, 96, 24), (1536, 120, 18)):
-        act(T.K[:, lo:lo + 16 * n], T.IO[:, 0:2016].indirect(T.off[:, o0:o0 + n]), [("IO", 0, 2016), ("off", o0, o0 + n)], [("K", lo, lo + 16 * n)])
-    tc(T.IE[:, 0:2016].indirect(T.off[:, 72:120]), T.vals[:, 0:768], [("off", 72, 120), ("vals", 0, 768)], [("IE", 0, 2016)])
-    ts(T.DMj[:, :], T.DMi[:, :], 15, None, A.bitwise_and, None, [("DMi", 0, C)], [("DMj", 0, C)])
-    ts(T.DM[:, :], T.DMj[:, :], 0.0, None, A.is_equal, None, [("DMj", 0, C)], [("DM", 0, C)])
-    diag("IE", 2016, "off", (120, 138))
-    tc(T.p1[:, :], T.cs[:, 15:C:16], [("cs", 0, C)], [("p1", 0, 18)])
-    ts(T.nA[:, :], T.p1[:, :], 768.0, -1.0, A.is_lt, A.mult, [("p1", 0, 18)], [("nA", 0, 18)])
-    ts(T.n2[:, :], T.p1[:, :], 1536.0, -1.0, A.is_lt, A.mult, [("p1", 0, 18)], [("n2", 0, 18)])
+        act(T.E[:, lo + 384:lo + 768], T.E[:, 2304:4608].indirect(T.off[:, 24 * s:24 * s + 24]), [("E", 2304, 4608), ("off", 24 * s, 24 * s + 24)], [("E", lo + 384, lo + 768)])
+    def table_e():
+        for s in range(3):
+            lo = 768 * s
+            act(T.E[:, lo + 96:lo + 384], T.E[:, lo + 480:lo + 768], [("E", lo + 480, lo + 768)], [("E", lo + 96, lo + 384)])
+
+    def table_k():
+        for lo, o0, n in ((384, 72, 24), (1152, 96, 24), (1536, 120, 18)):
+            act(T.K[:, lo:lo + 16 * n], T.IO[:, 0:2304].indirect(T.off[:, o0:o0 + n]), [("IO", 0, 2304), ("off", o0, o0 + n)], [("K", lo, lo + 16 * n)])
+        for lo in (0, 768):
+            act(T.K[:, lo + 96:lo + 384], T.K[:, lo + 480:lo + 768], [("K", lo + 480, lo + 768)], [("K", lo + 96, lo + 384)])
+
+    tc(T.IE[:, 0:2304].indirect(T.off[:, 72:120]), T.vals[:, 0:768], [("off", 72, 120), ("vals", 0, 768)], [("IE", 0, 2304)])
+    diag("IE", 2304, "off", (120, 138))
+    z1 = T.cs[:, 15:C:16]
+    ts(T.nA[:, :], z1, 768.0, -1.0, A.is_lt, A.mult, [("cs", 0, C)], [("nA", 0, 18)])
+    ts(T.n2[:, :], z1, 1536.0, -1.0, A.is_lt, A.mult, [("cs", 0, C)], [("n2", 0, 18)])
+    tc(T.TB1[:, 0:54:3], z1, [("cs", 0, C)], [("TB1", 0, 54, 1)])
     tt(T.nB[:, :], T.n2[:, :], T.nA[:, :], A.subtract, [("n2", 0, 18), ("nA", 0, 18)], [("nB", 0, 18)])
-    ts(T.n3[:, :], T.n2[:, :], -384.0, None, A.mult, None, [("n2", 0, 18)], [("n3", 0, 18)])
-    tt(T.TB1[:, 0:54:3], T.p1[:, :], T.n3[:, :], A.add, [("p1", 0, 18), ("n3", 0, 18)], [("TB1", 0, 54, 1)])
-    for lo in (0, 768):
-        tc(T.K[:, lo + 384:lo + 768], T.K[:, lo:lo + 384], [("K", lo, lo + 384)], [("K", lo + 384, lo + 768)])
 
     for t in range(ROUNDS):
         last = t == ROUNDS - 1
-        window()
+        if t == 0:
+            table_k()
+        window(t)
         lists()
         gather("G0", M0, 0, 8)
         gq, lq = "gq%d" % t, "lq%d" % t
@@ -362,10 +392,10 @@ def rank_program(g, core, T, topo):
         times32("zb", "Z1", 640)
         layer("zq1", M1, "zb", "rf1", "X1")
         quant("xq1", 0, M1, "X1", 0)
-        act(T.ca[:, t:24:3], T.cw[:, 0:8], [("cw", 0, 8)], [("ca", 0, 24)])
+        actb(T.ca[:, t:24:3], T.cw[:, 0:8], 384.0, [("cw", 0, 8)], [("ca", 0, 24)])
         if t == 0:
             for b in range(4):
-                quant("eq%d" % b, 0, 128, "big", 3 - b + 1664)
+                quant("eq%d" % b, 0, 128, "big", 3 - b + 1668)
         if last:
             dma("sy", "finc", T.ac[:, :], T.ca[0:1, :], [("ca", 0, 24)], [])
             quant("vq", 0, 128, "vt", 0)
@@ -376,6 +406,8 @@ def rank_program(g, core, T, topo):
             act(T.yt[:, M0:C], pv(k, M1), [pr(k)], [("yt", M0, C)])
             dma("sy", "fin1", T.y[:, M0:C], T.yt[:, M0:C], [("yt", M0, C)], [])
         else:
+            score(1)
+            score(2)
             early(t + 1)
         for b in range(4):
             k = mm("eq%d" % b, 0, lq, 0, M0)

from concourse.mybir import dt, AluOpType as A, ActivationFunctionType as F

C, M0, M1 = 288, 128, 160
ROUNDS = 3
MASK = [1, 2, 4]
SB = 160
BLK = 4 * SB
W1 = 7 * BLK
WIN = 14 * BLK
WLEN = WIN - 3 * SB
BF, FP, I32, U16, X4, U8 = "bfloat16", "float32", "int32", "uint16", "float8_e4m3fn_x4", "uint8"

SCRATCH = {"ps": ("psum", [128, 4096], FP)}


def _buf(n, name, d):
    SCRATCH[name] = ("sbuf", [128, n], d)


for _n, _w in (("xt", 4 * C), ("ut", 512), ("vt", 512), ("X0", 512), ("X1", 640), ("G0", 512), ("Z0", 512), ("Z1", 640), ("za", 512),
               ("zb", 640), ("it", 512), ("on", 512), ("big", 2184), ("win", WIN)):
    _buf(_w, _n, BF)
for _n, _w in (("uq", 128), ("vq", 128), ("xq0", 128), ("xq1", 160), ("zq0", 128), ("zq1", 160), ("iq", 128), ("oq", 128), ("wq", 512),
               ("cq0", 416), ("cq1", 416), ("cq2", 416), ("cq3", 416), ("eq0", 128), ("eq1", 128), ("eq2", 128), ("eq3", 128),
               ("gq0", 128), ("gq1", 128), ("gq2", 128), ("lq0", 128), ("lq1", 128), ("lq2", 128)):
    _buf(_w, _n, X4)
    _buf(_w, _n + "s", U8)
for _n, _w in (("rf0", 512), ("rf1", 640), ("RO", 120), ("RE", 120), ("rel", 120), ("vals", 1152), ("IO", 2304), ("IE", 2304), ("K", 1824),
               ("E", 4608), ("jj", 384), ("DM", C), ("RST", C), ("RST3", 54), ("RST4", 72), ("mk", C), ("cs", C), ("nA", 18), ("nB", 18),
               ("n2", 18), ("TB1", 54), ("sc1", 54), ("TB2", 72), ("sc2", 72), ("cw", 24), ("LB", 24), ("df", 4), ("pc", 4), ("sA", 8), ("sB", 8),
               ("yt", C), ("ca", 24)):
    _buf(_w, _n, FP)
for _n, _w in (("R", 144), ("pn", 12), ("own", 18), ("hh", 8), ("h2", 8), ("h3", 8), ("DMi", 16), ("DMj", 16)):
    _buf(_w, _n, I32)
for _n, _w in (("off", 138), ("offL", 2), ("off1", 18), ("off2", 18), ("off3", 18)):
    _buf(_w, _n, U16)

SEMAPHORES = ["spe", "sve", "sac", "sgp", "ldx", "ldu", "ldr", "ldw", "ldv", "sh0", "sh1", "sh2", "sw0", "sw1", "sw2", "fin1", "fin0", "finy",
              "finc", "ra0", "ra1", "ra2", "lsent"]


def rank_program(g, core, T, topo):
    rank = T.rank_of(core)
    if rank is None:
        return
    Q = {"pe": g.tensor, "ve": g.vector, "ac": g.scalar, "gp": g, "sy": g.sync}
    SEM = {"pe": "spe", "ve": "sve", "ac": "sac", "gp": "sgp"}
    count = {}
    known = {q: {} for q in Q}
    book = {}

    def touch(q, rd, wr):
        need = []
        for r, w in [(r, False) for r in rd] + [(r, True) for r in wr]:
            b, lo, hi, m = (tuple(r) + (15,))[:4]
            for (l2, h2, m2, w2, q2, tok) in book.get(b, []):
                if l2 < hi and lo < h2 and m & m2:
                    if w:
                        if q2 != q or w2: need.append(tok)
                    elif w2 or (b == "ps" and q2 != q):
                        need.append(tok)
        return need

    def settle(q, need):
        k = known[q]
        best = {}
        for t in need:
            if k.get(t[0], 0) < t[1] and (t[0] not in best or best[t[0]][1] < t[1]):
                best[t[0]] = t
        todo = list(best.values())
        todo = [t for t in todo if not any(u is not t and u[2].get(t[0], 0) >= t[1] for u in todo)]
        for t in todo:
            Q[q].wait_ge(T.sem[t[0]], t[1])
            k[t[0]] = max(k.get(t[0], 0), t[1])
            for s, v in t[2].items():
                k[s] = max(k.get(s, 0), v)

    def note(rd, wr, qtag, tok):
        for r in rd:
            b, lo, hi, m = (tuple(r) + (15,))[:4]
            book.setdefault(b, []).append((lo, hi, m, False, qtag, tok))
        for r in wr:
            b, lo, hi, m = (tuple(r) + (15,))[:4]
            book[b] = [e for e in book.get(b, []) if not (lo <= e[0] and e[1] <= hi and e[2] & m == e[2])]
            book[b].append((lo, hi, m, True, qtag, tok))

    def run(q, fn, rd, wr):
        settle(q, touch(q, rd, wr))
        s = SEM[q]
        fn(Q[q]).then_inc(T.sem[s], 1)
        count[s] = count.get(s, 0) + 1
        snap = dict(known[q])
        snap[s] = count[s]
        note(rd, wr, q, (s, count[s], snap))

    groups = {}

    def dma(q, grp, out, in_, rd, wr):
        settle(q, touch(None, rd, wr))
        Q[q].dma_start(out, in_).then_inc(T.sem[grp], 16)
        tok = groups.setdefault(grp, [grp, 0, {}])
        tok[1] += 16
        for s, v in known[q].items():
            tok[2][s] = max(tok[2].get(s, 0), v)
        count[grp] = tok[1]
        note(rd, wr, None, tok)

    def ts(out, in0, s1, s2, o0, o1, rd, wr):
        if o1 is None:
            run("ve", lambda e: e.tensor_scalar(out, in0, s1, s2, o0), rd, wr)
        else:
            run("ve", lambda e: e.tensor_scalar(out, in0, s1, s2, o0, o1), rd, wr)

    def tt(out, a, b, o, rd, wr):
        run("ve", lambda e: e.tensor_tensor(out, a, b, o), rd, wr)

    def tc(out, in_, rd, wr):
        run("ve", lambda e: e.tensor_copy(out, in_), rd, wr)

    def ms(b, c, lo, hi, step=1, p0=0, p1=128):
        run("ve", lambda e: e.memset(T[b][p0:p1, lo:hi:step], c), [], [(b, lo, hi)])

    def act(out, in_, rd, wr, scale=1.0):
        if scale == 1.0:
            run("ac", lambda e: e.activation(out, in_, F.Copy), rd, wr)
        else:
            run("ac", lambda e: e.activation(out, in_, F.Copy, scale=scale), rd, wr)

    def actb(out, in_, bias, rd, wr):
        run("ac", lambda e: e.activation(out, in_, F.Identity, bias=bias), rd, wr)

    def quant(q, lo, n, src, slo):
        run("ve", lambda e: e.quantize_mx(T[q][:, lo:lo + n], T[q + "s"][:, lo:lo + n], T[src][:, slo:slo + 4 * n]),
            [(src, slo, slo + 4 * n)], [(q, lo, lo + n), (q + "s", lo, lo + n)])

    bank = [0]

    def mm(st, slo, mv, mlo, n):
        b = bank[0]
        bank[0] = (b + 1) % 8
        o = T.ps[:, 512 * b:512 * b + n]
        run("pe", lambda e: e.matmul_mx(o, T[st][:, slo:slo + 128], T[st + "s"][:, slo:slo + 128], T[mv][:, mlo:mlo + n], T[mv + "s"][:, mlo:mlo + n], True, True),
            [(st, slo, slo + 128), (st + "s", slo, slo + 128), (mv, mlo, mlo + n), (mv + "s", mlo, mlo + n)], [("ps", 512 * b, 512 * b + 512)])
        return b

    def pr(b):
        return ("ps", 512 * b, 512 * b + 512)

    def pv(b, n):
        return T.ps[:, 512 * b:512 * b + n]

    def diag(src, width, offs, ocols):
        o0, o1 = ocols
        n = 16 * (o1 - o0)
        tt(T.mk[:, 0:n], T[src][:, 0:width].indirect(T[offs][:, o0:o1]), T.DM[:, 0:n], A.mult,
           [(src, 0, width), (offs, o0, o1), ("DM", 0, n)], [("mk", 0, n)])
        run("ve", lambda e: e.tensor_tensor_scan(T.cs[:, 0:n], T.RST[:, 0:n], T.mk[:, 0:n], 0.0, A.mult, A.add),
            [("RST", 0, n), ("mk", 0, n)], [("cs", 0, n)])

    dma("sy", "ldx", T.xt[:, :], T.x[:, :], [], [("xt", 0, 4 * C)])
    turn = 0
    for i, s in enumerate((-2, 0, 2, -1, 1, 3)):
        r = 16 * (s % 8)
        c0, c1 = 24 * i, 24 * i + 24
        for lo, hi, so in ((0, 128 - r, r), (128 - r, 128, r - 128)):
            if lo < hi:
                dma("sy" if turn % 4 else "ac", "ldr", T.R[lo:hi, c0:c1], T.ring[lo + so:hi + so, :], [], [("R", c0, c1, 1 if lo else 2)])
                turn += 1
    dma("sy", "ldu", T.ut[:, :], T.u[:, :], [], [("ut", 0, 512)])
    dma("sy", "ldw", T.wq[:, 0:512].bitcast(dt.uint8), T.wc[:, :], [], [("wq", 0, 512)])
    dma("sy", "ldw", T.wqs[:, 0:512], T.ws[:, :], [], [("wqs", 0, 512)])
    dma("sy", "ldv", T.vt[:, :], T.v[:, :], [], [("vt", 0, 512)])

    ms("big", 0.0, 0, 2184)
    run("gp", lambda e: e.iota(T.pn[:, 0:1], [[1, 1]], 0, 1), [], [("pn", 0, 1)])
    run("gp", lambda e: e.iota(T.DMi[:, :], [[1, 16]], 128, -1), [], [("DMi", 0, 16)])
    run("gp", lambda e: e.iota(T.jj[:, :], [[1, 384]], 0, 0, allow_small_or_imprecise_dtypes=True), [], [("jj", 0, 384)])
    run("gp", lambda e: e.iota(T.own[:, :], [[16, 18]], 0, 0), [], [("own", 0, 18)])
    run("gp", lambda e: e.iota(T.hh[:, :], [[1, 8]], 10, 0), [], [("hh", 0, 8)])

    def ones(c0, c1, pattern, base):
        v = T.big[:, 3 + 4 * c0:4 * c1:4]
        run("gp", lambda e: e.affine_select(v, v, pattern, A.not_equal, 1.0, base, -1), [("big", 4 * c0, 4 * c1)], [("big", 4 * c0, 4 * c1)])

    ones(0, 32, [[0, 2], [1, 16]], 96)
    ones(32, 160, [[32, 4], [0, 2], [1, 16]], 0)
    ones(160, 224, [[32, 2], [0, 2], [1, 16]], 0)
    ones(224, 256, [[0, 2], [1, 16]], 112)
    ones(256, 384, [[32, 4], [0, 2], [1, 16]], 16)
    ones(384, 416, [[0, 2], [1, 16]], 16)

    def count_up(b, lo, base):
        run("gp", lambda e: e.iota(T[b][:, lo:lo + C], [[1, C]], base, 0, allow_small_or_imprecise_dtypes=True), [], [(b, lo, lo + C)])

    for h in (0, 2, 4, 6):
        count_up("IO", C * h, 2304 + C * h)
    for h in (1, 3, 5, 7):
        count_up("IE", C * h, 1536)
    ones(417, 545, [[1, 128]], 0)

    def pn(i): return T.pn[:, i:i + 1]
    def pr_(i): return ("pn", i, i + 1)
    ts(T.DMj[:, :], T.DMi[:, :], 15, None, A.bitwise_and, None, [("DMi", 0, 16)], [("DMj", 0, 16)])
    ts(pn(1), pn(0), 4, 1, A.logical_shift_right, A.bitwise_and, [pr_(0)], [pr_(1)])
    ts(T.DM[:, 0:16], T.DMj[:, :], 0.0, None, A.is_equal, None, [("DMj", 0, 16)], [("DM", 0, 16)])
    ts(pn(2), pn(0), 15, None, A.bitwise_and, None, [pr_(0)], [pr_(2)])
    ts(pn(3), pn(0), 4, 6, A.logical_shift_right, A.bitwise_and, [pr_(0)], [pr_(3)])
    ts(pn(4), pn(0), 4, None, A.logical_shift_right, None, [pr_(0)], [pr_(4)])
    tc(T.pc[:, 0:1], pn(1), [pr_(1)], [("pc", 0, 1)])
    ts(T.pc[:, 1:2], pn(1), -1.0, 1.0, A.mult, A.add, [pr_(1)], [("pc", 1, 2)])
    ts(T.pc[:, 2:3], pn(3), -1.0, None, A.mult, None, [pr_(3)], [("pc", 2, 3)])
    ts(pn(5), pn(4), 288.0, None, A.mult, None, [pr_(4)], [pr_(5)])
    tt(pn(7), pn(3), pn(2), A.add, [pr_(3), pr_(2)], [pr_(7)])
    ts(pn(10), pn(2), 5.0, 16.0, A.is_ge, A.mult, [pr_(2)], [pr_(10)])
    ts(T.h2[:, :], T.hh[:, :], T.pc[:, 2:3], None, A.add, None, [("hh", 0, 8), ("pc", 2, 3)], [("h2", 0, 8)])
    tt(pn(6), pn(5), pn(2), A.add, [pr_(5), pr_(2)], [pr_(6)])
    ts(pn(8), pn(7), 7.0, None, A.add, None, [pr_(7)], [pr_(8)])
    ts(T.h3[:, :], T.h2[:, :], 7, None, A.bitwise_and, None, [("h2", 0, 8)], [("h3", 0, 8)])
    tc(T.pc[:, 3:4], pn(6), [pr_(6)], [("pc", 3, 4)])
    ts(pn(9), pn(8), 7, None, A.bitwise_and, None, [pr_(8)], [pr_(9)])
    ts(T.sA[:, :], T.h3[:, :], float(BLK), None, A.mult, None, [("h3", 0, 8)], [("sA", 0, 8)])
    ts(T.sB[:, :], T.h3[:, :], float(BLK), float(W1 - M0), A.mult, A.add, [("h3", 0, 8)], [("sB", 0, 8)])
    ts(T.off[:, 120:138], T.own[:, :], T.pc[:, 3:4], None, A.add, None, [("own", 0, 18), ("pc", 3, 4)], [("off", 120, 138)])
    tt(pn(11), pn(9), pn(10), A.add, [pr_(9), pr_(10)], [pr_(11)])
    ms("RST3", 1.0, 0, 54)
    tc(T.offL[:, 0:1], pn(11), [pr_(11)], [("offL", 0, 2)])
    ms("RST4", 1.0, 0, 72)
    ms("RST3", 0.0, 0, 54, 3)
    ms("RST4", 0.0, 0, 72, 4)
    ms("cw", 0.0, 0, 24)
    ms("LB", 0.0, 0, 24)

    def fill(b, lo, hi, c):
        for k in range(lo, hi, 384):
            n = min(384, hi - k)
            run("ac", lambda e: e.activation(T[b][:, k:k + n], T.jj[:, 0:n], F.Identity, bias=c, scale=0.0), [("jj", 0, n)], [(b, k, k + n)])

    fill("on", 0, 512, 1.0)
    run("ac", lambda e: e.activation(T.RST[:, 0:16], T.jj[:, 0:16], F.Sign), [("jj", 0, 16)], [("RST", 0, 16)])
    fill("it", 0, 512, 0.0)
    for lo, n in ((16, 16), (32, 32), (64, 64), (128, 128), (256, 32)):
        for b in ("DM", "RST"):
            act(T[b][:, lo:lo + n], T[b][:, 0:n], [(b, 0, n)], [(b, lo, lo + n)])
    for s in range(3):
        actb(T.vals[:, 384 * s:384 * s + 384], T.jj[:, :], 768.0 * s, [("jj", 0, 384)], [("vals", 384 * s, 384 * s + 384)])
    fill("win", 2 * BLK, 3 * BLK, 0.0)
    for h in range(8):
        lo = 2304 + C * h
        actb(T.E[:, lo:lo + M0], T.jj[:, 0:M0], T.sA[:, h:h + 1], [("jj", 0, M0), ("sA", h, h + 1)], [("E", lo, lo + M0)])
        actb(T.E[:, lo + M0:lo + C], T.jj[:, M0:C], T.sB[:, h:h + 1], [("jj", M0, C), ("sB", h, h + 1)], [("E", lo + M0, lo + C)])

    def score(blk):
        st, lo = (("xq0", 0), ("xq1", 0), ("xq1", 32))[blk]
        b = mm(st, lo, "uq", 0, 128)
        ts(T.it[:, blk:32:4], T.ps[:, 512 * b:512 * b + 128:16], 0.0, None, A.is_gt, None, [pr(b)], [("it", 0, 32, 1 << blk)])

    def unpack(D, b, q, n, where):
        lo = 32 * (D // 2) + (224 if D % 2 else 0)
        k = mm("cq%d" % b, lo, q, 0, n)
        at = where + BLK * D + SB * b
        act(T.win[:, at:at + n], pv(k, n), [pr(k)], [("win", at, at + n)])

    def spread(sem, base, blocks):
        src = base + 2 * BLK
        for dst, n, sh in blocks:
            r = sh % 128
            d0 = base + dst
            for lo, hi, so in ((0, 128 - r, r), (128 - r, 128, r - 128)):
                dma("sy", sem, T.win[lo:hi, d0:d0 + n], T.win[lo + so:hi + so, src:src + n],
                    [("win", src, src + n)], [("win", d0, d0 + n, 1 if lo else 2)])

    def early(t):
        for D in (2, 3):
            for b in range(4):
                unpack(D, b, "xq1", M1, W1)
        spread("sh%d" % t, W1, ((0, 2 * BLK, -32), (4 * BLK, 2 * BLK, 32), (6 * BLK, BLK, 64)))

    def add_up():
        k = mm("oq", 0, "iq", 0, 128)
        ts(T.cw[:, 0:8], pv(k, 8), -384.0, None, A.add, None, [pr(k)], [("cw", 0, 8)])

    def window(t):
        if t:
            score(0)
            quant("iq", 0, 128, "it", 0)
        i = 0
        for D in (2, 3, 1, 4, 5, 6):
            for b in range(4):
                unpack(D, b, "xq0", M0, 0)
                i += 1
                if i == (2 if t else 8):
                    add_up()
            if D == 2:
                spread("sw%d" % t, 0, ((0, BLK, -32),))
                if t == 0:
                    table_e()

    def lists():
        tc(T.LB[:, 2:18], T.cw[:, 0:24].indirect(T.offL[:, 0:1]), [("cw", 0, 24), ("offL", 0, 2)], [("LB", 2, 18)])
        ts(T.TB1[:, 1:54:3], T.nA[:, :], T.LB[:, 3:4], None, A.mult, None, [("nA", 0, 18), ("LB", 3, 4)], [("TB1", 0, 54, 2)])
        ts(T.TB1[:, 2:54:3], T.nB[:, :], T.LB[:, 5:6], None, A.mult, None, [("nB", 0, 18), ("LB", 5, 6)], [("TB1", 0, 54, 4)])
        tt(T.df[:, :], T.LB[:, 0:8:2], T.LB[:, 2:10:2], A.subtract, [("LB", 0, 10)], [("df", 0, 4)])
        run("ve", lambda e: e.tensor_tensor_scan(T.sc1[:, :], T.RST3[:, :], T.TB1[:, :], 0.0, A.mult, A.add), [("RST3", 0, 54), ("TB1", 0, 54)], [("sc1", 0, 54)])
        tc(T.off1[:, :], T.sc1[:, 2:54:3], [("sc1", 0, 54)], [("off1", 0, 18)])
        diag("K", 1824, "off1", (0, 18))
        z = T.cs[:, 15:C:16]
        ts(T.TB2[:, 0:72:4], z, T.df[:, 0:1], None, A.add, None, [("cs", 0, C), ("df", 0, 1)], [("TB2", 0, 72, 1)])
        for i in (1, 2, 3):
            ts(T.TB2[:, i:72:4], z, 768.0 * i, T.df[:, i:i + 1], A.is_ge, A.mult, [("cs", 0, C), ("df", i, i + 1)], [("TB2", 0, 72, 1 << i)])
        run("ve", lambda e: e.tensor_tensor_scan(T.sc2[:, :], T.RST4[:, :], T.TB2[:, :], 0.0, A.mult, A.add), [("RST4", 0, 72), ("TB2", 0, 72)], [("sc2", 0, 72)])
        tc(T.off2[:, :], T.sc2[:, 3:72:4], [("sc2", 0, 72)], [("off2", 0, 18)])
        diag("E", 4608, "off2", (0, 18))
        tc(T.off3[:, :], T.cs[:, 15:C:16], [("cs", 0, C)], [("off3", 0, 18)])

    def gather(dst, n, o0, o1):
        for b in (0, 2, 1, 3):
            o = T[dst][:, b:4 * n:4]
            i = T.win[:, SB * b:SB * b + WLEN].indirect(T.off3[:, o0:o1])
            (tc if b < 2 else act)(o, i, [("win", SB * b, SB * b + WLEN), ("off3", o0, o1)], [(dst, 0, 4 * n, 1 << b)])

    def layer(zq, n, z32, rf, X):
        for b in range(4):
            k = mm("wq", 128 * b, zq, 0, n)
            lo = n * b
            tt(T[rf][:, lo:lo + n], pv(k, n), T[z32][:, b:4 * n:4], A.add, [pr(k), (z32, 0, 4 * n)], [(rf, lo, lo + n)])
            act(T[X][:, b:4 * n:4], T[rf][:, lo:lo + n], [(rf, lo, lo + n)], [(X, 0, 4 * n, 1 << b)], scale=0.03125)

    def times32(dst, src, n):
        ts(T[dst][:, 0:n], T[src][:, 0:n], 32.0, None, A.mult, None, [(src, 0, n)], [(dst, 0, n)])

    ms("on", 0.0, 2, 512, 4, 0, 96)
    quant("oq", 0, 128, "on", 0)
    quant("cq0", 0, 416, "big", 3)
    quant("cq1", 0, 416, "big", 2)
    quant("xq1", 0, M1, "xt", 512)
    quant("xq0", 0, M0, "xt", 0)
    quant("cq2", 0, 416, "big", 1)
    quant("cq3", 0, 416, "big", 0)
    early(0)
    ts(T.RO[:, :], T.R[:, 0:120], T.pc[:, 0:1], None, A.mult, None, [("R", 0, 120), ("pc", 0, 1)], [("RO", 0, 120)])
    ts(T.RE[:, 0:72], T.R[:, 72:144], T.pc[:, 1:2], None, A.mult, None, [("R", 72, 144), ("pc", 1, 2)], [("RE", 0, 72)])
    ts(T.RE[:, 72:120], T.R[:, 24:72], T.pc[:, 1:2], None, A.mult, None, [("R", 24, 72), ("pc", 1, 2)], [("RE", 72, 120)])
    tt(T.rel[:, :], T.RO[:, :], T.RE[:, :], A.add, [("RO", 0, 120), ("RE", 0, 120)], [("rel", 0, 120)])
    tc(T.off[:, 0:120], T.rel[:, :], [("rel", 0, 120)], [("off", 0, 120)])
    quant("uq", 0, 128, "ut", 0)
    tc(T.IO[:, 0:2304].indirect(T.off[:, 0:72]), T.vals[:, :], [("off", 0, 72), ("vals", 0, 1152)], [("IO", 0, 2304)])
    for k in (1, 2, 0):
        score(k)
    quant("iq", 0, 128, "it", 0)
    for s in range(3):
        lo = 768 * s
        act(T.E[:, lo + 384:lo + 768], T.E[:, 2304:4608].indirect(T.off[:, 24 * s:24 * s + 24]), [("E", 2304, 4608), ("off", 24 * s, 24 * s + 24)], [("E", lo + 384, lo + 768)])
    def table_e():
        for s in range(3):
            lo = 768 * s
            act(T.E[:, lo + 96:lo + 384], T.E[:, lo + 480:lo + 768], [("E", lo + 480, lo + 768)], [("E", lo + 96, lo + 384)])

    def table_k():
        for lo, o0, n in ((384, 72, 24), (1152, 96, 24), (1536, 120, 18)):
            act(T.K[:, lo:lo + 16 * n], T.IO[:, 0:2304].indirect(T.off[:, o0:o0 + n]), [("IO", 0, 2304), ("off", o0, o0 + n)], [("K", lo, lo + 16 * n)])
        for lo in (0, 768):
            act(T.K[:, lo + 96:lo + 384], T.K[:, lo + 480:lo + 768], [("K", lo + 480, lo + 768)], [("K", lo + 96, lo + 384)])

    tc(T.IE[:, 0:2304].indirect(T.off[:, 72:120]), T.vals[:, 0:768], [("off", 72, 120), ("vals", 0, 768)], [("IE", 0, 2304)])
    diag("IE", 2304, "off", (120, 138))
    z1 = T.cs[:, 15:C:16]
    ts(T.nA[:, :], z1, 768.0, -1.0, A.is_lt, A.mult, [("cs", 0, C)], [("nA", 0, 18)])
    ts(T.n2[:, :], z1, 1536.0, -1.0, A.is_lt, A.mult, [("cs", 0, C)], [("n2", 0, 18)])
    tc(T.TB1[:, 0:54:3], z1, [("cs", 0, C)], [("TB1", 0, 54, 1)])
    tt(T.nB[:, :], T.n2[:, :], T.nA[:, :], A.subtract, [("n2", 0, 18), ("nA", 0, 18)], [("nB", 0, 18)])

    for t in range(ROUNDS):
        last = t == ROUNDS - 1
        if t == 0:
            table_k()
        window(t)
        lists()
        gather("G0", M0, 0, 8)
        gq, lq = "gq%d" % t, "lq%d" % t
        quant(gq, 0, M0, "G0", 0)
        dst = T.cores[rank ^ MASK[t]]
        rid, pid = topo.addr(dst, core)
        mask, ne = topo.mask(core, dst), len(topo.engines(core, dst))
        settle("gp", touch("gp", [(gq, 0, M0), (gq + "s", 0, M0)], []))
        for o, i in ((T[lq][:, 0:M0].bitcast(dt.uint8), T[gq][:, 0:M0].bitcast(dt.uint8)), (T[lq + "s"][:, 0:M0], T[gq + "s"][:, 0:M0])):
            g.remote_dma(out_ap=o, in_ap=i, remote_sem=T.sem["ra%d" % t], local_sem=T.sem.lsent, pid=pid, routing_id=rid, dma_engine_mask=mask)
        count["ra%d" % t] = 2 * ne
        count["lsent"] = count.get("lsent", 0) + 2 * ne
        note([], [(lq, 0, M0), (lq + "s", 0, M0)], None, ("ra%d" % t, 2 * ne, {}))
        gather("Z1", M1, 8, 18)
        quant("zq1", 0, M1, "Z1", 0)
        times32("zb", "Z1", 640)
        layer("zq1", M1, "zb", "rf1", "X1")
        quant("xq1", 0, M1, "X1", 0)
        actb(T.ca[:, t:24:3], T.cw[:, 0:8], 384.0, [("cw", 0, 8)], [("ca", 0, 24)])
        if t == 0:
            for b in range(4):
                quant("eq%d" % b, 0, 128, "big", 3 - b + 1668)
        if last:
            dma("sy", "finc", T.ac[:, :], T.ca[0:1, :], [("ca", 0, 24)], [])
            quant("vq", 0, 128, "vt", 0)
            dma("sy", "fin1", T.oc[:, 512:1152], T.xq1[:, :].bitcast(dt.uint8), [("xq1", 0, M1)], [])
            for k in range(4):
                dma("sy", "fin1", T.osc[4 * k:4 * k + 4, M0:C], T.xq1s[32 * k:32 * k + 4, :], [("xq1s", 0, M1)], [])
            k = mm("vq", 0, "xq1", 0, M1)
            act(T.yt[:, M0:C], pv(k, M1), [pr(k)], [("yt", M0, C)])
            dma("sy", "fin1", T.y[:, M0:C], T.yt[:, M0:C], [("yt", M0, C)], [])
        else:
            score(1)
            score(2)
            early(t + 1)
        for b in range(4):
            k = mm("eq%d" % b, 0, lq, 0, M0)
            (tc if b % 2 == 0 else act)(T.Z0[:, b:512:4], pv(k, M0), [pr(k)], [("Z0", 0, 512, 1 << b)])
        quant("zq0", 0, M0, "Z0", 0)
        times32("za", "Z0", 512)
        layer("zq0", M0, "za", "rf0", "X0")
        quant("xq0", 0, M0, "X0", 0)
    dma("sy", "fin0", T.oc[:, 0:512], T.xq0[:, :].bitcast(dt.uint8), [("xq0", 0, M0)], [])
    for k in range(4):
        dma("sy", "fin0", T.osc[4 * k:4 * k + 4, 0:M0], T.xq0s[32 * k:32 * k + 4, :], [("xq0s", 0, M0)], [])
    k = mm("vq", 0, "xq0", 0, M0)
    act(T.yt[:, 0:M0], pv(k, M0), [pr(k)], [("yt", 0, M0)])
    dma("ac", "finy", T.y[:, 0:M0], T.yt[:, 0:M0], [("yt", 0, M0)], [])
    for s, v in count.items():
        g.wait_ge(T.sem[s], v)
